import numpy as np
import ml_dtypes


def mxq(x, axis, fmt="e4m3"):
    dtype, down = {"e4m3": (ml_dtypes.float8_e4m3fn, 7), "e5m2": (ml_dtypes.float8_e5m2, 14)}[fmt]
    v = np.moveaxis(np.asarray(x, np.float32).astype(ml_dtypes.bfloat16).astype(np.float64), axis, -1)
    blocks = v.reshape(v.shape[:-1] + (-1, 32))
    amax = np.abs(blocks).max(-1, keepdims=True)
    byte = np.maximum(np.where(amax > 0, np.frexp(amax)[1] - 1 + 127, 0) - down, 1)
    scale = np.exp2(byte - 127.0)
    codes = (blocks / scale).astype(np.float32).astype(dtype).astype(np.float64)
    return np.moveaxis((codes * scale).reshape(v.shape), -1, axis)


WIDE = False


def mx_kscale(k):
    if not WIDE:
        return np.ones(k)
    levels = np.array([10, -10, 5, -5, 0])
    if k % 512:
        return np.exp2(np.random.permutation(np.resize(levels, k // 32))).repeat(32)
    a = np.empty((k // 512, 16))
    for p in range(k // 512):
        a[p, :8] = np.random.permutation(np.resize(levels, 8))
        for g in range(8):
            far = levels[np.abs(levels - a[p, g]) >= 10]
            a[p, g + 8] = far[np.random.randint(len(far))]
    return np.exp2(a.ravel()).repeat(32)


def f64(x):
    return np.asarray(x).astype(np.float64)


def striped(idx):
    return np.tile(idx.reshape(-1, 16).T, (8, 1)).astype(np.uint16)


def unstriped(offs):
    return offs[:16].T.reshape(-1).astype(np.int64)


E2M1 = np.array([0.0, 0.5, 1.0, 1.5, 2.0, 3.0, 4.0, 6.0, -0.0, -0.5, -1.0, -1.5, -2.0, -3.0, -4.0, -6.0])


def pack_weight(w, fmt):
    k, n = w.shape
    w = f64(np.asarray(w, np.float32).astype(ml_dtypes.bfloat16)).reshape(k // 32, 32, n)
    amax = np.abs(w).max(1)
    if fmt == "e4m3":
        byte = np.frexp(amax)[1] - 1 + 127 - 7
    else:
        mant, ex = np.frexp(amax / 6.0)
        byte = np.where(mant > 0.5, ex, ex - 1) + 127
    byte = np.clip(np.where(amax > 0, byte, 1), 1, 254)
    scaled = (w * np.exp2(127.0 - byte)[:, None, :]).reshape(k, n).astype(np.float32)
    by_word = np.ascontiguousarray(scaled.reshape(k // 512, 128, 4, n).transpose(0, 1, 3, 2))
    if fmt == "e4m3":
        words = by_word.astype(ml_dtypes.float8_e4m3fn).view(np.uint8)
    else:
        c = by_word.astype(ml_dtypes.float4_e2m1fn).view(np.uint8) & 0xF
        words = (c[..., 0::2] | (c[..., 1::2] << 4)).reshape(k // 512, 128, 2 * n)
    return np.ascontiguousarray(words), np.ascontiguousarray(byte.astype(np.uint8).reshape(k // 512, 16, n))


def unpack_weight(words, scales, fmt):
    g, _, n = scales.shape
    words = np.ascontiguousarray(words).reshape(g, 128, n, -1)
    if fmt == "e4m3":
        vals = words.view(ml_dtypes.float8_e4m3fn).astype(np.float64)
    else:
        nib = np.empty((g, 128, n, 4), np.uint8)
        nib[..., 0::2] = words & 0xF
        nib[..., 1::2] = words >> 4
        vals = E2M1[nib]
    vals = vals * np.repeat(np.exp2(scales.astype(np.float64) - 127.0), 8, axis=1)[..., None]
    return vals.transpose(0, 1, 3, 2).reshape(g * 512, n)


def pack_table(v):
    words, scales = pack_weight(v, "e4m3")
    return np.concatenate([words.reshape(words.shape[0], -1), scales.reshape(scales.shape[0], -1)], axis=1)


def unpack_table(tab):
    g, t = tab.shape[0], tab.shape[1] // 528
    return unpack_weight(tab[:, :512 * t].reshape(g, 128, t, 4), tab[:, 512 * t:].reshape(g, 16, t), "e4m3")


K, M, T, S = 512, 512, 2048, 1024


def setup_inputs():
    n = np.random.standard_normal
    s = mx_kscale(K)[:, None]
    return {
        "tab": pack_table(n((K, T)) * s),
        "w": (n((K, M)) / np.sqrt(K) / s).astype(np.float32),
        "wgo": np.tile(np.random.uniform(0.5, 2.0, S), (128, 1)).astype(np.float32),
        "offs": striped(np.random.permutation(T)[:S]),
        "offs2": striped(np.random.permutation(T)[:S]),
    }


def reference(tab, w, wgo, offs, offs2):
    tab_ = unpack_table(tab)[:, unstriped(offs)]
    w_ = mxq(f64(w), 0, "e4m3")
    y = w_.T @ tab_
    out = np.zeros((M, T))
    out[:, unstriped(offs2)] = f64(wgo)[0] * (y)
    return out

@@ -1,0 +1,111 @@
+from contextlib import ExitStack
+
+import concourse.mybir as mybir
+
+K, M, T, S = 512, 512, 2048, 1024
+FLOPS = 2 * K * M * S
+
+F32 = mybir.dt.float32
+BF16 = mybir.dt.bfloat16
+I32 = mybir.dt.int32
+U32 = mybir.dt.uint32
+U16 = mybir.dt.uint16
+U8 = mybir.dt.uint8
+FP8X4 = mybir.dt.float8_e4m3fn_x4
+MULT = mybir.AluOpType.mult
+
+P = 128
+PACK = 4
+
+
+def tile_list_tabscat_none_kernel(tc, tab, w, wgo, offs, offs2, out):
+    nc = tc.nc
+    with ExitStack() as ctx:
+        held = ctx.enter_context(tc.tile_pool(name="held", bufs=1))
+        psum = ctx.enter_context(tc.psum_pool(name="psum", bufs=1))
+
+        offsets = held.tile([P, S // 16], U16, name="offsets")
+        offsets2 = held.tile([P, S // 16], U16, name="offsets2")
+        scales = held.tile([P, T // 4], I32, name="scales", align_bytes=64)
+        words = held.tile([P, T], I32, name="words", align_bytes=64)
+        picked_words = held.tile([P, S], U32, name="picked_words", align_bytes=64)
+        picked_scales = held.tile([P, S], U8, name="picked_scales", align_bytes=64)
+        weights = held.tile([P, S], F32, name="weights")
+        windows = [held.tile([P, T], F32, name=f"window{b}") for b in range(2)]
+
+        nc.gpsimd.memset(scales[:], 0)
+        nc.vector.memset(windows[0][:], 0.0)
+        nc.gpsimd.memset(windows[1][:], 0.0)
+
+        tab_words = tab[0, 0 : K * T].rearrange("(p b) -> p b", p=P).bitcast(I32)
+        tab_scales = tab[0, K * T : K * T + 16 * T].rearrange("(q t) -> q t", q=16).bitcast(I32)
+        w_rows = w.rearrange("(p j) c -> p j c", j=PACK)
+        w_chunks = ((0, 256), (256, 512))
+        raws = [held.tile([P, PACK, c1 - c0], F32, name=f"raw{c0}") for c0, c1 in w_chunks]
+
+        def load_w(i):
+            nc.sync.dma_start(out=raws[i][:], in_=w_rows[:, :, w_chunks[i][0] : w_chunks[i][1]])
+
+        nc.sync.dma_start(offsets[:], offs)
+
+        for q in range(4):
+            nc.sync.dma_start(out=scales[32 * q : 32 * q + 4, :], in_=tab_scales[4 * q : 4 * q + 4, :])
+        load_w(0)
+        load_w(1)
+        nc.sync.dma_start(out=words[:], in_=tab_words)
+        nc.sync.dma_start(offsets2[:], offs2)
+        nc.sync.dma_start(out=weights[:], in_=wgo)
+
+        codes = held.tile([P, M], U32, name="codes", align_bytes=64)
+        planes = held.tile([P, M], U8, name="planes", align_bytes=64)
+        grouped = held.tile([P, M, PACK], BF16, name="grouped", align_bytes=64)
+
+        def prepare_w(i, a, b):
+            c0 = w_chunks[i][0]
+            nc.scalar.copy(out=grouped[:, a:b, :], in_=raws[i][:, :, a - c0 : b - c0].rearrange("p j c -> p c j"))
+            nc.vector.quantize_mx(
+                out=codes[:, a:b].bitcast(FP8X4),
+                scales=planes[:, a:b],
+                in_=grouped[:, a:b, :].rearrange("p c j -> p (c j)"),
+            )
+
+        def pick(dst, src, a, b):
+            nc.vector.tensor_copy(out=dst[:, a:b], in_=src.indirect(offsets[:, a // 16 : b // 16]))
+
+        banks = [0]
+
+        def product(m, y, a, b):
+            acc = psum.tile([P, b - a], F32, name=f"acc{banks[0] % 8}")
+            banks[0] += 1
+            nc.tensor.matmul_mx(
+                out=acc[:],
+                lhsT=codes[:, m * P : (m + 1) * P].bitcast(FP8X4),
+                lhsT_scale=planes[:, m * P : (m + 1) * P],
+                rhs=picked_words[:, a:b].bitcast(FP8X4),
+                rhs_scale=picked_scales[:, a:b],
+                start=True,
+                stop=True,
+            )
+            nc.scalar.copy(out=y[:, a:b], in_=acc[:])
+
+        def place(m, y, a, b):
+            nc.vector.tensor_tensor(
+                windows[m % 2][:].indirect(offsets2[:, a // 16 : b // 16]), y[:, a:b], weights[:, a:b], MULT
+            )
+
+        pieces = ((0, 256), (256, 1024))
+        pick(picked_scales, scales[:].bitcast(U8), 0, S)
+        prepare_w(0, 0, 256)
+        prepare_w(1, 256, 512)
+        ys = [held.tile([P, S], F32, name=f"y{m}") for m in range(4)]
+        for a, b in pieces:
+            pick(picked_words, words[:].bitcast(U32), a, b)
+            for c in range(a, b, 512):
+                product(0, ys[0], c, min(c + 512, b))
+        for m in range(4):
+            if m > 0:
+                for a, b in ((0, 512), (512, 1024)):
+                    product(m, ys[m], a, b)
+            for a, b in pieces if m == 0 else ((0, S),):
+                place(m, ys[m], a, b)
+            nc.sync.dma_start(out=out[m * P : (m + 1) * P, :], in_=windows[m % 2][:])

@@ -16,6 +16,8 @@ MULT = mybir.AluOpType.mult
 
 P = 128
 PACK = 4
+HALF = S // 2
+FIRST = 256
 
 
 def tile_list_tabscat_none_kernel(tc, tab, w, wgo, offs, offs2, out):
@@ -28,60 +30,62 @@ def tile_list_tabscat_none_kernel(tc, tab, w, wgo, offs, offs2, out):
         offsets2 = held.tile([P, S // 16], U16, name="offsets2")
         scales = held.tile([P, T // 4], I32, name="scales", align_bytes=64)
         words = held.tile([P, T], I32, name="words", align_bytes=64)
-        picked_words = held.tile([P, S], U32, name="picked_words", align_bytes=64)
         picked_scales = held.tile([P, S], U8, name="picked_scales", align_bytes=64)
         weights = held.tile([P, S], F32, name="weights")
         windows = [held.tile([P, T], F32, name=f"window{b}") for b in range(2)]
 
-        nc.gpsimd.memset(scales[:], 0)
+        nc.vector.memset(scales[:, 0:352], 0)
+        nc.gpsimd.memset(scales[:, 352 : T // 4], 0)
         nc.vector.memset(windows[0][:], 0.0)
         nc.gpsimd.memset(windows[1][:], 0.0)
 
         tab_words = tab[0, 0 : K * T].rearrange("(p b) -> p b", p=P).bitcast(I32)
         tab_scales = tab[0, K * T : K * T + 16 * T].rearrange("(q t) -> q t", q=16).bitcast(I32)
         w_rows = w.rearrange("(p j) c -> p j c", j=PACK)
-        w_chunks = ((0, 256), (256, 512))
+        w_chunks = ((0, 128), (128, 512))
         raws = [held.tile([P, PACK, c1 - c0], F32, name=f"raw{c0}") for c0, c1 in w_chunks]
 
         def load_w(i):
             nc.sync.dma_start(out=raws[i][:], in_=w_rows[:, :, w_chunks[i][0] : w_chunks[i][1]])
 
         nc.sync.dma_start(offsets[:], offs)
-
+        nc.sync.dma_start(offsets2[:], offs2)
         for q in range(4):
             nc.sync.dma_start(out=scales[32 * q : 32 * q + 4, :], in_=tab_scales[4 * q : 4 * q + 4, :])
-        load_w(0)
-        load_w(1)
         nc.sync.dma_start(out=words[:], in_=tab_words)
-        nc.sync.dma_start(offsets2[:], offs2)
-        nc.sync.dma_start(out=weights[:], in_=wgo)
+        load_w(0)
+        nc.sync.dma_start(out=weights[:, 0:FIRST], in_=wgo[:, 0:FIRST])
+        load_w(1)
+        nc.sync.dma_start(out=weights[:, FIRST:S], in_=wgo[:, FIRST:S])
 
         codes = held.tile([P, M], U32, name="codes", align_bytes=64)
         planes = held.tile([P, M], U8, name="planes", align_bytes=64)
-        grouped = held.tile([P, M, PACK], BF16, name="grouped", align_bytes=64)
 
-        def prepare_w(i, a, b):
+        def prepare_w(i, a, b, tag):
             c0 = w_chunks[i][0]
-            nc.scalar.copy(out=grouped[:, a:b, :], in_=raws[i][:, :, a - c0 : b - c0].rearrange("p j c -> p c j"))
+            grouped = held.tile([P, b - a, PACK], BF16, name=f"grouped{a}", tag=tag, align_bytes=64)
+            nc.scalar.copy(out=grouped[:], in_=raws[i][:, :, a - c0 : b - c0].rearrange("p j c -> p c j"))
             nc.vector.quantize_mx(
                 out=codes[:, a:b].bitcast(FP8X4),
                 scales=planes[:, a:b],
-                in_=grouped[:, a:b, :].rearrange("p c j -> p (c j)"),
+                in_=grouped[:].rearrange("p c j -> p (c j)"),
             )
 
         def pick(dst, src, a, b):
-            nc.vector.tensor_copy(out=dst[:, a:b], in_=src.indirect(offsets[:, a // 16 : b // 16]))
+            nc.vector.tensor_copy(out=dst, in_=src.indirect(offsets[:, a // 16 : b // 16]))
 
         banks = [0]
+        picked = []
 
         def product(m, y, a, b):
             acc = psum.tile([P, b - a], F32, name=f"acc{banks[0] % 8}")
             banks[0] += 1
+            h = a // HALF
             nc.tensor.matmul_mx(
                 out=acc[:],
                 lhsT=codes[:, m * P : (m + 1) * P].bitcast(FP8X4),
                 lhsT_scale=planes[:, m * P : (m + 1) * P],
-                rhs=picked_words[:, a:b].bitcast(FP8X4),
+                rhs=picked[h][:, a - h * HALF : b - h * HALF].bitcast(FP8X4),
                 rhs_scale=picked_scales[:, a:b],
                 start=True,
                 stop=True,
@@ -93,19 +97,22 @@ def tile_list_tabscat_none_kernel(tc, tab, w, wgo, offs, offs2, out):
                 windows[m % 2][:].indirect(offsets2[:, a // 16 : b // 16]), y[:, a:b], weights[:, a:b], MULT
             )
 
-        pieces = ((0, 256), (256, 1024))
-        pick(picked_scales, scales[:].bitcast(U8), 0, S)
-        prepare_w(0, 0, 256)
-        prepare_w(1, 256, 512)
         ys = [held.tile([P, S], F32, name=f"y{m}") for m in range(4)]
-        for a, b in pieces:
-            pick(picked_words, words[:].bitcast(U32), a, b)
-            for c in range(a, b, 512):
-                product(0, ys[0], c, min(c + 512, b))
+        pick(picked_scales[:], scales[:].bitcast(U8), 0, S)
+        picked.append(held.tile([P, HALF], U32, name="picked0", align_bytes=64))
+        pick(picked[0][:], words[:].bitcast(U32), 0, HALF)
+        prepare_w(0, 0, P, "staged")
+        product(0, ys[0], 0, FIRST)
+        picked.append(held.tile([P, HALF], U32, name="picked1", tag="staged", align_bytes=64))
+        pick(picked[1][:], words[:].bitcast(U32), HALF, S)
+        product(0, ys[0], FIRST, HALF)
+        product(0, ys[0], HALF, S)
+        place(0, ys[0], 0, FIRST)
+        prepare_w(1, P, 2 * P, "grouped1")
+        prepare_w(1, 2 * P, M, "grouped2")
         for m in range(4):
             if m > 0:
-                for a, b in ((0, 512), (512, 1024)):
+                for a, b in ((0, HALF), (HALF, S)):
                     product(m, ys[m], a, b)
-            for a, b in pieces if m == 0 else ((0, S),):
-                place(m, ys[m], a, b)
+            place(m, ys[m], FIRST if m == 0 else 0, S)
             nc.sync.dma_start(out=out[m * P : (m + 1) * P, :], in_=windows[m % 2][:])

@@ -32,12 +32,10 @@ def tile_list_tabscat_none_kernel(tc, tab, w, wgo, offs, offs2, out):
         words = held.tile([P, T], I32, name="words", align_bytes=64)
         picked_scales = held.tile([P, S], U8, name="picked_scales", align_bytes=64)
         weights = held.tile([P, S], F32, name="weights")
-        windows = [held.tile([P, T], F32, name=f"window{b}") for b in range(2)]
+        windows = [held.tile([P, T], F32, name="window0", align_bytes=64)]
 
-        nc.vector.memset(scales[:, 0:352], 0)
-        nc.gpsimd.memset(scales[:, 352 : T // 4], 0)
+        nc.vector.memset(scales[:, 0:512], 0)
         nc.vector.memset(windows[0][:], 0.0)
-        nc.gpsimd.memset(windows[1][:], 0.0)
 
         tab_words = tab[0, 0 : K * T].rearrange("(p b) -> p b", p=P).bitcast(I32)
         tab_scales = tab[0, K * T : K * T + 16 * T].rearrange("(q t) -> q t", q=16).bitcast(I32)
@@ -51,7 +49,8 @@ def tile_list_tabscat_none_kernel(tc, tab, w, wgo, offs, offs2, out):
         nc.sync.dma_start(offsets[:], offs)
         nc.sync.dma_start(offsets2[:], offs2)
         for q in range(4):
-            nc.sync.dma_start(out=scales[32 * q : 32 * q + 4, :], in_=tab_scales[4 * q : 4 * q + 4, :])
+            queue = nc.sync if q % 2 else nc.scalar
+            queue.dma_start(out=scales[32 * q : 32 * q + 4, :], in_=tab_scales[4 * q : 4 * q + 4, :])
         nc.sync.dma_start(out=words[:], in_=tab_words)
         load_w(0)
         nc.sync.dma_start(out=weights[:, 0:FIRST], in_=wgo[:, 0:FIRST])
@@ -110,6 +109,8 @@ def tile_list_tabscat_none_kernel(tc, tab, w, wgo, offs, offs2, out):
         place(0, ys[0], 0, FIRST)
         prepare_w(1, P, 2 * P, "grouped1")
         prepare_w(1, 2 * P, M, "grouped2")
+        windows.append(held.tile([P, T], F32, name="window1", tag="grouped2", align_bytes=64))
+        nc.gpsimd.memset(windows[1][:], 0.0)
         for m in range(4):
             if m > 0:
                 for a, b in ((0, HALF), (HALF, S)):

@@ -17,7 +17,7 @@ MULT = mybir.AluOpType.mult
 P = 128
 PACK = 4
 HALF = S // 2
-FIRST = 256
+FIRST = 384
 
 
 def tile_list_tabscat_none_kernel(tc, tab, w, wgo, offs, offs2, out):
@@ -47,12 +47,13 @@ def tile_list_tabscat_none_kernel(tc, tab, w, wgo, offs, offs2, out):
             nc.sync.dma_start(out=raws[i][:], in_=w_rows[:, :, w_chunks[i][0] : w_chunks[i][1]])
 
         nc.sync.dma_start(offsets[:], offs)
-        nc.sync.dma_start(offsets2[:], offs2)
+        nc.sync.dma_start(out=words[:, 0:512], in_=tab_words[:, 0:512])
         for q in range(4):
             queue = nc.sync if q % 2 else nc.scalar
             queue.dma_start(out=scales[32 * q : 32 * q + 4, :], in_=tab_scales[4 * q : 4 * q + 4, :])
-        nc.sync.dma_start(out=words[:], in_=tab_words)
+        nc.sync.dma_start(out=words[:, 512:T], in_=tab_words[:, 512:T])
         load_w(0)
+        nc.sync.dma_start(offsets2[:], offs2)
         nc.sync.dma_start(out=weights[:, 0:FIRST], in_=wgo[:, 0:FIRST])
         load_w(1)
         nc.sync.dma_start(out=weights[:, FIRST:S], in_=wgo[:, FIRST:S])
@@ -79,12 +80,12 @@ def tile_list_tabscat_none_kernel(tc, tab, w, wgo, offs, offs2, out):
         def product(m, y, a, b):
             acc = psum.tile([P, b - a], F32, name=f"acc{banks[0] % 8}")
             banks[0] += 1
-            h = a // HALF
+            h = 0 if a < FIRST else 1
             nc.tensor.matmul_mx(
                 out=acc[:],
                 lhsT=codes[:, m * P : (m + 1) * P].bitcast(FP8X4),
                 lhsT_scale=planes[:, m * P : (m + 1) * P],
-                rhs=picked[h][:, a - h * HALF : b - h * HALF].bitcast(FP8X4),
+                rhs=picked[h][:, a - h * FIRST : b - h * FIRST].bitcast(FP8X4),
                 rhs_scale=picked_scales[:, a:b],
                 start=True,
                 stop=True,
@@ -98,22 +99,23 @@ def tile_list_tabscat_none_kernel(tc, tab, w, wgo, offs, offs2, out):
 
         ys = [held.tile([P, S], F32, name=f"y{m}") for m in range(4)]
         pick(picked_scales[:], scales[:].bitcast(U8), 0, S)
-        picked.append(held.tile([P, HALF], U32, name="picked0", align_bytes=64))
-        pick(picked[0][:], words[:].bitcast(U32), 0, HALF)
+        picked.append(held.tile([P, FIRST], U32, name="picked0", align_bytes=64))
+        pick(picked[0][:], words[:].bitcast(U32), 0, FIRST)
         prepare_w(0, 0, P, "staged")
-        product(0, ys[0], 0, FIRST)
-        picked.append(held.tile([P, HALF], U32, name="picked1", tag="staged", align_bytes=64))
-        pick(picked[1][:], words[:].bitcast(U32), HALF, S)
-        product(0, ys[0], FIRST, HALF)
-        product(0, ys[0], HALF, S)
+        product(0, ys[0], 0, 256)
+        product(0, ys[0], 256, FIRST)
+        picked.append(held.tile([P, S - FIRST], U32, name="picked1", tag="staged", align_bytes=64))
+        pick(picked[1][:], words[:].bitcast(U32), FIRST, S)
+        product(0, ys[0], FIRST, FIRST + HALF)
+        product(0, ys[0], FIRST + HALF, S)
         place(0, ys[0], 0, FIRST)
         prepare_w(1, P, 2 * P, "grouped1")
-        prepare_w(1, 2 * P, M, "grouped2")
-        windows.append(held.tile([P, T], F32, name="window1", tag="grouped2", align_bytes=64))
+        windows.append(held.tile([P, T], F32, name="window1", tag="grouped1", align_bytes=64))
         nc.gpsimd.memset(windows[1][:], 0.0)
+        prepare_w(1, 2 * P, M, "grouped2")
         for m in range(4):
             if m > 0:
-                for a, b in ((0, HALF), (HALF, S)):
+                for a, b in ((0, 256), (256, FIRST), (FIRST, FIRST + HALF), (FIRST + HALF, S)):
                     product(m, ys[m], a, b)
             place(m, ys[m], FIRST if m == 0 else 0, S)
             nc.sync.dma_start(out=out[m * P : (m + 1) * P, :], in_=windows[m % 2][:])

@@ -40,23 +40,22 @@ def tile_list_tabscat_none_kernel(tc, tab, w, wgo, offs, offs2, out):
         tab_words = tab[0, 0 : K * T].rearrange("(p b) -> p b", p=P).bitcast(I32)
         tab_scales = tab[0, K * T : K * T + 16 * T].rearrange("(q t) -> q t", q=16).bitcast(I32)
         w_rows = w.rearrange("(p j) c -> p j c", j=PACK)
-        w_chunks = ((0, 128), (128, 512))
+        w_chunks = ((0, 128), (128, 256), (256, 512))
         raws = [held.tile([P, PACK, c1 - c0], F32, name=f"raw{c0}") for c0, c1 in w_chunks]
 
         def load_w(i):
             nc.sync.dma_start(out=raws[i][:], in_=w_rows[:, :, w_chunks[i][0] : w_chunks[i][1]])
 
+        nc.scalar.dma_start(out=words[:, 0:512], in_=tab_words[:, 0:512])
         nc.sync.dma_start(offsets[:], offs)
-        nc.sync.dma_start(out=words[:, 0:512], in_=tab_words[:, 0:512])
+        nc.sync.dma_start(offsets2[:], offs2)
         for q in range(4):
-            queue = nc.sync if q % 2 else nc.scalar
-            queue.dma_start(out=scales[32 * q : 32 * q + 4, :], in_=tab_scales[4 * q : 4 * q + 4, :])
+            nc.sync.dma_start(out=scales[32 * q : 32 * q + 4, :], in_=tab_scales[4 * q : 4 * q + 4, :])
         nc.sync.dma_start(out=words[:, 512:T], in_=tab_words[:, 512:T])
         load_w(0)
-        nc.sync.dma_start(offsets2[:], offs2)
-        nc.sync.dma_start(out=weights[:, 0:FIRST], in_=wgo[:, 0:FIRST])
         load_w(1)
-        nc.sync.dma_start(out=weights[:, FIRST:S], in_=wgo[:, FIRST:S])
+        nc.sync.dma_start(out=weights[:], in_=wgo)
+        load_w(2)
 
         codes = held.tile([P, M], U32, name="codes", align_bytes=64)
         planes = held.tile([P, M], U8, name="planes", align_bytes=64)
@@ -110,9 +109,9 @@ def tile_list_tabscat_none_kernel(tc, tab, w, wgo, offs, offs2, out):
         product(0, ys[0], FIRST + HALF, S)
         place(0, ys[0], 0, FIRST)
         prepare_w(1, P, 2 * P, "grouped1")
-        windows.append(held.tile([P, T], F32, name="window1", tag="grouped1", align_bytes=64))
+        prepare_w(2, 2 * P, M, "grouped2")
+        windows.append(held.tile([P, T], F32, name="window1", tag="grouped2", align_bytes=64))
         nc.gpsimd.memset(windows[1][:], 0.0)
-        prepare_w(1, 2 * P, M, "grouped2")
         for m in range(4):
             if m > 0:
                 for a, b in ((0, 256), (256, FIRST), (FIRST, FIRST + HALF), (FIRST + HALF, S)):

@@ -63,7 +63,10 @@ def tile_list_tabscat_none_kernel(tc, tab, w, wgo, offs, offs2, out):
         def prepare_w(i, a, b, tag):
             c0 = w_chunks[i][0]
             grouped = held.tile([P, b - a, PACK], BF16, name=f"grouped{a}", tag=tag, align_bytes=64)
-            nc.scalar.copy(out=grouped[:], in_=raws[i][:, :, a - c0 : b - c0].rearrange("p j c -> p c j"))
+            nc.scalar.copy(
+                out=grouped[:].rearrange("p (c e) j -> p c j e", e=2),
+                in_=raws[i][:, :, a - c0 : b - c0].rearrange("p j (c e) -> p c j e", e=2),
+            )
             nc.vector.quantize_mx(
                 out=codes[:, a:b].bitcast(FP8X4),
                 scales=planes[:, a:b],

@@ -49,8 +49,8 @@ def tile_list_tabscat_none_kernel(tc, tab, w, wgo, offs, offs2, out):
         nc.scalar.dma_start(out=words[:, 0:512], in_=tab_words[:, 0:512])
         nc.sync.dma_start(offsets[:], offs)
         nc.sync.dma_start(offsets2[:], offs2)
-        for q in range(4):
-            nc.sync.dma_start(out=scales[32 * q : 32 * q + 4, :], in_=tab_scales[4 * q : 4 * q + 4, :])
+        for r in range(4):
+            nc.sync.dma_start(out=scales[r:P:32, :], in_=tab_scales[r:16:4, :])
         nc.sync.dma_start(out=words[:, 512:T], in_=tab_words[:, 512:T])
         load_w(0)
         load_w(1)

@@ -17,7 +17,7 @@ MULT = mybir.AluOpType.mult
 P = 128
 PACK = 4
 HALF = S // 2
-FIRST = 384
+FIRST = 256
 
 
 def tile_list_tabscat_none_kernel(tc, tab, w, wgo, offs, offs2, out):
@@ -46,12 +46,12 @@ def tile_list_tabscat_none_kernel(tc, tab, w, wgo, offs, offs2, out):
         def load_w(i):
             nc.sync.dma_start(out=raws[i][:], in_=w_rows[:, :, w_chunks[i][0] : w_chunks[i][1]])
 
-        nc.scalar.dma_start(out=words[:, 0:512], in_=tab_words[:, 0:512])
+        nc.scalar.dma_start(out=words[:, 0:384], in_=tab_words[:, 0:384])
         nc.sync.dma_start(offsets[:], offs)
         nc.sync.dma_start(offsets2[:], offs2)
         for r in range(4):
             nc.sync.dma_start(out=scales[r:P:32, :], in_=tab_scales[r:16:4, :])
-        nc.sync.dma_start(out=words[:, 512:T], in_=tab_words[:, 512:T])
+        nc.sync.dma_start(out=words[:, 384:T], in_=tab_words[:, 384:T])
         load_w(0)
         load_w(1)
         nc.sync.dma_start(out=weights[:], in_=wgo)
@@ -82,12 +82,12 @@ def tile_list_tabscat_none_kernel(tc, tab, w, wgo, offs, offs2, out):
         def product(m, y, a, b):
             acc = psum.tile([P, b - a], F32, name=f"acc{banks[0] % 8}")
             banks[0] += 1
-            h = 0 if a < FIRST else 1
+            h = a // HALF
             nc.tensor.matmul_mx(
                 out=acc[:],
                 lhsT=codes[:, m * P : (m + 1) * P].bitcast(FP8X4),
                 lhsT_scale=planes[:, m * P : (m + 1) * P],
-                rhs=picked[h][:, a - h * FIRST : b - h * FIRST].bitcast(FP8X4),
+                rhs=picked[h][:, a - h * HALF : b - h * HALF].bitcast(FP8X4),
                 rhs_scale=picked_scales[:, a:b],
                 start=True,
                 stop=True,
@@ -101,15 +101,14 @@ def tile_list_tabscat_none_kernel(tc, tab, w, wgo, offs, offs2, out):
 
         ys = [held.tile([P, S], F32, name=f"y{m}") for m in range(4)]
         pick(picked_scales[:], scales[:].bitcast(U8), 0, S)
-        picked.append(held.tile([P, FIRST], U32, name="picked0", align_bytes=64))
-        pick(picked[0][:], words[:].bitcast(U32), 0, FIRST)
+        picked.append(held.tile([P, HALF], U32, name="picked0", align_bytes=64))
+        pick(picked[0][:], words[:].bitcast(U32), 0, HALF)
         prepare_w(0, 0, P, "staged")
-        product(0, ys[0], 0, 256)
-        product(0, ys[0], 256, FIRST)
-        picked.append(held.tile([P, S - FIRST], U32, name="picked1", tag="staged", align_bytes=64))
-        pick(picked[1][:], words[:].bitcast(U32), FIRST, S)
-        product(0, ys[0], FIRST, FIRST + HALF)
-        product(0, ys[0], FIRST + HALF, S)
+        product(0, ys[0], 0, FIRST)
+        product(0, ys[0], FIRST, HALF)
+        picked.append(held.tile([P, HALF], U32, name="picked1", tag="staged", align_bytes=64))
+        pick(picked[1][:], words[:].bitcast(U32), HALF, S)
+        product(0, ys[0], HALF, S)
         place(0, ys[0], 0, FIRST)
         prepare_w(1, P, 2 * P, "grouped1")
         prepare_w(2, 2 * P, M, "grouped2")
@@ -117,7 +116,7 @@ def tile_list_tabscat_none_kernel(tc, tab, w, wgo, offs, offs2, out):
         nc.gpsimd.memset(windows[1][:], 0.0)
         for m in range(4):
             if m > 0:
-                for a, b in ((0, 256), (256, FIRST), (FIRST, FIRST + HALF), (FIRST + HALF, S)):
+                for a, b in ((0, HALF), (HALF, S)):
                     product(m, ys[m], a, b)
             place(m, ys[m], FIRST if m == 0 else 0, S)
             nc.sync.dma_start(out=out[m * P : (m + 1) * P, :], in_=windows[m % 2][:])

@@ -17,7 +17,8 @@ MULT = mybir.AluOpType.mult
 P = 128
 PACK = 4
 HALF = S // 2
-FIRST = 256
+FIRST = 384
+ROW0 = 112
 
 
 def tile_list_tabscat_none_kernel(tc, tab, w, wgo, offs, offs2, out):
@@ -28,34 +29,33 @@ def tile_list_tabscat_none_kernel(tc, tab, w, wgo, offs, offs2, out):
 
         offsets = held.tile([P, S // 16], U16, name="offsets")
         offsets2 = held.tile([P, S // 16], U16, name="offsets2")
-        scales = held.tile([P, T // 4], I32, name="scales", align_bytes=64)
+        scales = held.tile([P, T // 4], I32, name="scales", tag="scales", align_bytes=64)
         words = held.tile([P, T], I32, name="words", align_bytes=64)
         picked_scales = held.tile([P, S], U8, name="picked_scales", align_bytes=64)
-        weights = held.tile([P, S], F32, name="weights")
+        weights_first = held.tile([P, FIRST], F32, name="weights_first")
         windows = [held.tile([P, T], F32, name="window0", align_bytes=64)]
 
-        nc.vector.memset(scales[:, 0:512], 0)
+        nc.vector.memset(scales[0:ROW0, :], 0)
+        nc.vector.memset(picked_scales[:].bitcast(I32), 0)
         nc.vector.memset(windows[0][:], 0.0)
 
         tab_words = tab[0, 0 : K * T].rearrange("(p b) -> p b", p=P).bitcast(I32)
         tab_scales = tab[0, K * T : K * T + 16 * T].rearrange("(q t) -> q t", q=16).bitcast(I32)
         w_rows = w.rearrange("(p j) c -> p j c", j=PACK)
         w_chunks = ((0, 128), (128, 256), (256, 512))
-        raws = [held.tile([P, PACK, c1 - c0], F32, name=f"raw{c0}") for c0, c1 in w_chunks]
+        raws = []
 
-        def load_w(i):
-            nc.sync.dma_start(out=raws[i][:], in_=w_rows[:, :, w_chunks[i][0] : w_chunks[i][1]])
+        def load_w(i, queue, tag):
+            c0, c1 = w_chunks[i]
+            raws.append(held.tile([P, PACK, c1 - c0], F32, name=f"raw{c0}", tag=tag, align_bytes=64))
+            queue.dma_start(out=raws[i][:], in_=w_rows[:, :, c0:c1])
 
-        nc.scalar.dma_start(out=words[:, 0:384], in_=tab_words[:, 0:384])
+        nc.scalar.dma_start(out=scales[ROW0:P, :], in_=tab_scales)
         nc.sync.dma_start(offsets[:], offs)
         nc.sync.dma_start(offsets2[:], offs2)
-        for r in range(4):
-            nc.sync.dma_start(out=scales[r:P:32, :], in_=tab_scales[r:16:4, :])
-        nc.sync.dma_start(out=words[:, 384:T], in_=tab_words[:, 384:T])
-        load_w(0)
-        load_w(1)
-        nc.sync.dma_start(out=weights[:], in_=wgo)
-        load_w(2)
+        nc.scalar.dma_start(out=words[:], in_=tab_words)
+        load_w(0, nc.scalar, "raw0")
+        nc.scalar.dma_start(out=weights_first[:], in_=wgo[:, 0:FIRST])
 
         codes = held.tile([P, M], U32, name="codes", align_bytes=64)
         planes = held.tile([P, M], U8, name="planes", align_bytes=64)
@@ -94,29 +94,45 @@ def tile_list_tabscat_none_kernel(tc, tab, w, wgo, offs, offs2, out):
             )
             nc.scalar.copy(out=y[:, a:b], in_=acc[:])
 
-        def place(m, y, a, b):
-            nc.vector.tensor_tensor(
-                windows[m % 2][:].indirect(offsets2[:, a // 16 : b // 16]), y[:, a:b], weights[:, a:b], MULT
-            )
+        def pick_scales(a, b, tag):
+            rows = held.tile([P, b - a], U8, name=f"rows{a}", tag=tag, align_bytes=64)
+            pick(rows[:], scales[:].bitcast(U8), a, b)
+            for r in range(4):
+                nc.sync.dma_start(
+                    out=picked_scales[r:P:32, a:b].bitcast(I32), in_=rows[ROW0 + r : P : 4, :].bitcast(I32)
+                )
 
-        ys = [held.tile([P, S], F32, name=f"y{m}") for m in range(4)]
-        pick(picked_scales[:], scales[:].bitcast(U8), 0, S)
+        ys = [held.tile([P, S], F32, name="y0")]
+        pick_scales(0, FIRST, "rows_first")
+        pick_scales(FIRST, S, "rows_rest")
+        load_w(1, nc.sync, "scales")
+        weights = held.tile([P, S], F32, name="weights", tag="rows_first", align_bytes=64)
+        nc.sync.dma_start(out=weights[:], in_=wgo)
+
         picked.append(held.tile([P, HALF], U32, name="picked0", align_bytes=64))
         pick(picked[0][:], words[:].bitcast(U32), 0, HALF)
         prepare_w(0, 0, P, "staged")
-        product(0, ys[0], 0, FIRST)
+        load_w(2, nc.sync, "raw0")
+        product(0, ys[0], 0, 256)
+        product(0, ys[0], 256, FIRST)
         product(0, ys[0], FIRST, HALF)
         picked.append(held.tile([P, HALF], U32, name="picked1", tag="staged", align_bytes=64))
         pick(picked[1][:], words[:].bitcast(U32), HALF, S)
         product(0, ys[0], HALF, S)
-        place(0, ys[0], 0, FIRST)
+        nc.vector.tensor_tensor(
+            windows[0][:].indirect(offsets2[:, 0 : FIRST // 16]), ys[0][:, 0:FIRST], weights_first[:], MULT
+        )
         prepare_w(1, P, 2 * P, "grouped1")
-        prepare_w(2, 2 * P, M, "grouped2")
-        windows.append(held.tile([P, T], F32, name="window1", tag="grouped2", align_bytes=64))
+        windows.append(held.tile([P, T], F32, name="window1", tag="grouped1", align_bytes=64))
         nc.gpsimd.memset(windows[1][:], 0.0)
+        prepare_w(2, 2 * P, M, "grouped2")
         for m in range(4):
+            a = FIRST if m == 0 else 0
             if m > 0:
-                for a, b in ((0, HALF), (HALF, S)):
-                    product(m, ys[m], a, b)
-            place(m, ys[m], FIRST if m == 0 else 0, S)
+                ys.append(held.tile([P, S], F32, name=f"y{m}", tag="raw0" if m == 1 else f"y{m}", align_bytes=64))
+                product(m, ys[m], 0, HALF)
+                product(m, ys[m], HALF, S)
+            nc.vector.tensor_tensor(
+                windows[m % 2][:].indirect(offsets2[:, a // 16 : S // 16]), ys[m][:, a:S], weights[:, a:S], MULT
+            )
             nc.sync.dma_start(out=out[m * P : (m + 1) * P, :], in_=windows[m % 2][:])

@@ -53,8 +53,8 @@ def tile_list_tabscat_none_kernel(tc, tab, w, wgo, offs, offs2, out):
         nc.scalar.dma_start(out=scales[ROW0:P, :], in_=tab_scales)
         nc.sync.dma_start(offsets[:], offs)
         nc.sync.dma_start(offsets2[:], offs2)
-        nc.scalar.dma_start(out=words[:], in_=tab_words)
         load_w(0, nc.scalar, "raw0")
+        nc.scalar.dma_start(out=words[:], in_=tab_words)
         nc.scalar.dma_start(out=weights_first[:], in_=wgo[:, 0:FIRST])
 
         codes = held.tile([P, M], U32, name="codes", align_bytes=64)
@@ -77,17 +77,15 @@ def tile_list_tabscat_none_kernel(tc, tab, w, wgo, offs, offs2, out):
             nc.vector.tensor_copy(out=dst, in_=src.indirect(offsets[:, a // 16 : b // 16]))
 
         banks = [0]
-        picked = []
 
         def product(m, y, a, b):
             acc = psum.tile([P, b - a], F32, name=f"acc{banks[0] % 8}")
             banks[0] += 1
-            h = a // HALF
             nc.tensor.matmul_mx(
                 out=acc[:],
                 lhsT=codes[:, m * P : (m + 1) * P].bitcast(FP8X4),
                 lhsT_scale=planes[:, m * P : (m + 1) * P],
-                rhs=picked[h][:, a - h * HALF : b - h * HALF].bitcast(FP8X4),
+                rhs=picked[:, a:b].bitcast(FP8X4),
                 rhs_scale=picked_scales[:, a:b],
                 start=True,
                 stop=True,
@@ -108,16 +106,15 @@ def tile_list_tabscat_none_kernel(tc, tab, w, wgo, offs, offs2, out):
         load_w(1, nc.sync, "scales")
         weights = held.tile([P, S], F32, name="weights", tag="rows_first", align_bytes=64)
         nc.sync.dma_start(out=weights[:], in_=wgo)
+        load_w(2, nc.sync, "rows_rest")
 
-        picked.append(held.tile([P, HALF], U32, name="picked0", align_bytes=64))
-        pick(picked[0][:], words[:].bitcast(U32), 0, HALF)
         prepare_w(0, 0, P, "staged")
-        load_w(2, nc.sync, "raw0")
+        picked = held.tile([P, S], U32, name="picked", tag="staged", align_bytes=64)
+        pick(picked[:, 0:FIRST], words[:].bitcast(U32), 0, FIRST)
         product(0, ys[0], 0, 256)
         product(0, ys[0], 256, FIRST)
+        pick(picked[:, FIRST:S], words[:].bitcast(U32), FIRST, S)
         product(0, ys[0], FIRST, HALF)
-        picked.append(held.tile([P, HALF], U32, name="picked1", tag="staged", align_bytes=64))
-        pick(picked[1][:], words[:].bitcast(U32), HALF, S)
         product(0, ys[0], HALF, S)
         nc.vector.tensor_tensor(
             windows[0][:].indirect(offsets2[:, 0 : FIRST // 16]), ys[0][:, 0:FIRST], weights_first[:], MULT
@@ -129,7 +126,7 @@ def tile_list_tabscat_none_kernel(tc, tab, w, wgo, offs, offs2, out):
         for m in range(4):
             a = FIRST if m == 0 else 0
             if m > 0:
-                ys.append(held.tile([P, S], F32, name=f"y{m}", tag="raw0" if m == 1 else f"y{m}", align_bytes=64))
+                ys.append(held.tile([P, S], F32, name=f"y{m}", tag="rows_rest" if m == 1 else f"y{m}", align_bytes=64))
                 product(m, ys[m], 0, HALF)
                 product(m, ys[m], HALF, S)
             nc.vector.tensor_tensor(

@@ -53,8 +53,11 @@ def tile_list_tabscat_none_kernel(tc, tab, w, wgo, offs, offs2, out):
         nc.scalar.dma_start(out=scales[ROW0:P, :], in_=tab_scales)
         nc.sync.dma_start(offsets[:], offs)
         nc.sync.dma_start(offsets2[:], offs2)
-        load_w(0, nc.scalar, "raw0")
+        first_rows = [held.tile([P, 2, P], F32, name=f"first_rows{u}") for u in range(2)]
+        raws.append(None)
+        nc.scalar.dma_start(out=first_rows[0][:], in_=w_rows[:, 0:2, 0:P])
         nc.scalar.dma_start(out=words[:], in_=tab_words)
+        nc.scalar.dma_start(out=first_rows[1][:], in_=w_rows[:, 2:4, 0:P])
         nc.scalar.dma_start(out=weights_first[:], in_=wgo[:, 0:FIRST])
 
         codes = held.tile([P, M], U32, name="codes", align_bytes=64)
@@ -63,10 +66,17 @@ def tile_list_tabscat_none_kernel(tc, tab, w, wgo, offs, offs2, out):
         def prepare_w(i, a, b, tag):
             c0 = w_chunks[i][0]
             grouped = held.tile([P, b - a, PACK], BF16, name=f"grouped{a}", tag=tag, align_bytes=64)
-            nc.scalar.copy(
-                out=grouped[:].rearrange("p (c e) j -> p c j e", e=2),
-                in_=raws[i][:, :, a - c0 : b - c0].rearrange("p j (c e) -> p c j e", e=2),
-            )
+            if i == 0:
+                for u in range(2):
+                    nc.scalar.copy(
+                        out=grouped[:, :, 2 * u : 2 * u + 2].rearrange("p (c e) j -> p c j e", e=2),
+                        in_=first_rows[u][:].rearrange("p j (c e) -> p c j e", e=2),
+                    )
+            else:
+                nc.scalar.copy(
+                    out=grouped[:].rearrange("p (c e) j -> p c j e", e=2),
+                    in_=raws[i][:, :, a - c0 : b - c0].rearrange("p j (c e) -> p c j e", e=2),
+                )
             nc.vector.quantize_mx(
                 out=codes[:, a:b].bitcast(FP8X4),
                 scales=planes[:, a:b],
@@ -77,15 +87,17 @@ def tile_list_tabscat_none_kernel(tc, tab, w, wgo, offs, offs2, out):
             nc.vector.tensor_copy(out=dst, in_=src.indirect(offsets[:, a // 16 : b // 16]))
 
         banks = [0]
+        picked = []
 
         def product(m, y, a, b):
             acc = psum.tile([P, b - a], F32, name=f"acc{banks[0] % 8}")
             banks[0] += 1
+            h = 0 if a < FIRST else 1
             nc.tensor.matmul_mx(
                 out=acc[:],
                 lhsT=codes[:, m * P : (m + 1) * P].bitcast(FP8X4),
                 lhsT_scale=planes[:, m * P : (m + 1) * P],
-                rhs=picked[:, a:b].bitcast(FP8X4),
+                rhs=picked[h][:, a - h * FIRST : b - h * FIRST].bitcast(FP8X4),
                 rhs_scale=picked_scales[:, a:b],
                 start=True,
                 stop=True,
@@ -108,14 +120,15 @@ def tile_list_tabscat_none_kernel(tc, tab, w, wgo, offs, offs2, out):
         nc.sync.dma_start(out=weights[:], in_=wgo)
         load_w(2, nc.sync, "rows_rest")
 
+        picked.append(held.tile([P, FIRST], U32, name="picked0", align_bytes=64))
+        pick(picked[0][:], words[:].bitcast(U32), 0, FIRST)
         prepare_w(0, 0, P, "staged")
-        picked = held.tile([P, S], U32, name="picked", tag="staged", align_bytes=64)
-        pick(picked[:, 0:FIRST], words[:].bitcast(U32), 0, FIRST)
         product(0, ys[0], 0, 256)
         product(0, ys[0], 256, FIRST)
-        pick(picked[:, FIRST:S], words[:].bitcast(U32), FIRST, S)
-        product(0, ys[0], FIRST, HALF)
-        product(0, ys[0], HALF, S)
+        picked.append(held.tile([P, S - FIRST], U32, name="picked1", tag="staged", align_bytes=64))
+        pick(picked[1][:], words[:].bitcast(U32), FIRST, S)
+        product(0, ys[0], FIRST, FIRST + HALF)
+        product(0, ys[0], FIRST + HALF, S)
         nc.vector.tensor_tensor(
             windows[0][:].indirect(offsets2[:, 0 : FIRST // 16]), ys[0][:, 0:FIRST], weights_first[:], MULT
         )
@@ -127,8 +140,8 @@ def tile_list_tabscat_none_kernel(tc, tab, w, wgo, offs, offs2, out):
             a = FIRST if m == 0 else 0
             if m > 0:
                 ys.append(held.tile([P, S], F32, name=f"y{m}", tag="rows_rest" if m == 1 else f"y{m}", align_bytes=64))
-                product(m, ys[m], 0, HALF)
-                product(m, ys[m], HALF, S)
+                for c, d in ((0, 256), (256, FIRST), (FIRST, FIRST + HALF), (FIRST + HALF, S)):
+                    product(m, ys[m], c, d)
             nc.vector.tensor_tensor(
                 windows[m % 2][:].indirect(offsets2[:, a // 16 : S // 16]), ys[m][:, a:S], weights[:, a:S], MULT
             )

@@ -32,7 +32,6 @@ def tile_list_tabscat_none_kernel(tc, tab, w, wgo, offs, offs2, out):
         scales = held.tile([P, T // 4], I32, name="scales", tag="scales", align_bytes=64)
         words = held.tile([P, T], I32, name="words", align_bytes=64)
         picked_scales = held.tile([P, S], U8, name="picked_scales", align_bytes=64)
-        weights_first = held.tile([P, FIRST], F32, name="weights_first")
         windows = [held.tile([P, T], F32, name="window0", align_bytes=64)]
 
         nc.vector.memset(scales[0:ROW0, :], 0)
@@ -53,12 +52,11 @@ def tile_list_tabscat_none_kernel(tc, tab, w, wgo, offs, offs2, out):
         nc.scalar.dma_start(out=scales[ROW0:P, :], in_=tab_scales)
         nc.sync.dma_start(offsets[:], offs)
         nc.sync.dma_start(offsets2[:], offs2)
-        first_rows = [held.tile([P, 2, P], F32, name=f"first_rows{u}") for u in range(2)]
+        first_rows = [held.tile([P, 2, P], F32, name=f"first_rows{u}", tag=f"first_rows{u}", align_bytes=64) for u in range(2)]
         raws.append(None)
         nc.scalar.dma_start(out=first_rows[0][:], in_=w_rows[:, 0:2, 0:P])
         nc.scalar.dma_start(out=words[:], in_=tab_words)
         nc.scalar.dma_start(out=first_rows[1][:], in_=w_rows[:, 2:4, 0:P])
-        nc.scalar.dma_start(out=weights_first[:], in_=wgo[:, 0:FIRST])
 
         codes = held.tile([P, M], U32, name="codes", align_bytes=64)
         planes = held.tile([P, M], U8, name="planes", align_bytes=64)
@@ -107,22 +105,28 @@ def tile_list_tabscat_none_kernel(tc, tab, w, wgo, offs, offs2, out):
         def pick_scales(a, b, tag):
             rows = held.tile([P, b - a], U8, name=f"rows{a}", tag=tag, align_bytes=64)
             pick(rows[:], scales[:].bitcast(U8), a, b)
+            return rows
+
+        def carry(rows, a, b):
             for r in range(4):
                 nc.sync.dma_start(
                     out=picked_scales[r:P:32, a:b].bitcast(I32), in_=rows[ROW0 + r : P : 4, :].bitcast(I32)
                 )
 
         ys = [held.tile([P, S], F32, name="y0")]
-        pick_scales(0, FIRST, "rows_first")
-        pick_scales(FIRST, S, "rows_rest")
-        load_w(1, nc.sync, "scales")
-        weights = held.tile([P, S], F32, name="weights", tag="rows_first", align_bytes=64)
-        nc.sync.dma_start(out=weights[:], in_=wgo)
-        load_w(2, nc.sync, "rows_rest")
+        carry(pick_scales(0, FIRST, "rows_first"), 0, FIRST)
+        rows_rest = pick_scales(FIRST, S, "rows_rest")
+        weights_first = held.tile([P, FIRST], F32, name="weights_first", tag="scales", align_bytes=64)
+        nc.sync.dma_start(out=weights_first[:], in_=wgo[:, 0:FIRST])
+        carry(rows_rest, FIRST, S)
+        load_w(1, nc.sync, "rows_first")
 
         picked.append(held.tile([P, FIRST], U32, name="picked0", align_bytes=64))
         pick(picked[0][:], words[:].bitcast(U32), 0, FIRST)
         prepare_w(0, 0, P, "staged")
+        weights = held.tile([P, S], F32, name="weights", tag="first_rows1", align_bytes=64)
+        nc.sync.dma_start(out=weights[:], in_=wgo)
+        load_w(2, nc.sync, "rows_rest")
         product(0, ys[0], 0, 256)
         product(0, ys[0], 256, FIRST)
         picked.append(held.tile([P, S - FIRST], U32, name="picked1", tag="staged", align_bytes=64))

@@ -124,12 +124,12 @@ def tile_list_tabscat_none_kernel(tc, tab, w, wgo, offs, offs2, out):
         picked.append(held.tile([P, FIRST], U32, name="picked0", align_bytes=64))
         pick(picked[0][:], words[:].bitcast(U32), 0, FIRST)
         prepare_w(0, 0, P, "staged")
-        weights = held.tile([P, S], F32, name="weights", tag="first_rows1", align_bytes=64)
+        weights = held.tile([P, S], F32, name="weights", tag="staged", align_bytes=64)
         nc.sync.dma_start(out=weights[:], in_=wgo)
         load_w(2, nc.sync, "rows_rest")
-        product(0, ys[0], 0, 256)
-        product(0, ys[0], 256, FIRST)
-        picked.append(held.tile([P, S - FIRST], U32, name="picked1", tag="staged", align_bytes=64))
+        for a in range(0, FIRST, P):
+            product(0, ys[0], a, a + P)
+        picked.append(held.tile([P, S - FIRST], U32, name="picked1", tag="first_rows1", align_bytes=64))
         pick(picked[1][:], words[:].bitcast(U32), FIRST, S)
         product(0, ys[0], FIRST, FIRST + HALF)
         product(0, ys[0], FIRST + HALF, S)

@@ -49,7 +49,7 @@ def tile_list_tabscat_none_kernel(tc, tab, w, wgo, offs, offs2, out):
             raws.append(held.tile([P, PACK, c1 - c0], F32, name=f"raw{c0}", tag=tag, align_bytes=64))
             queue.dma_start(out=raws[i][:], in_=w_rows[:, :, c0:c1])
 
-        nc.scalar.dma_start(out=scales[ROW0:P, :], in_=tab_scales)
+        nc.sync.dma_start(out=scales[ROW0:P, :], in_=tab_scales)
         nc.sync.dma_start(offsets[:], offs)
         nc.sync.dma_start(offsets2[:], offs2)
         first_rows = [held.tile([P, 2, P], F32, name=f"first_rows{u}", tag=f"first_rows{u}", align_bytes=64) for u in range(2)]

@@ -17,7 +17,7 @@ MULT = mybir.AluOpType.mult
 P = 128
 PACK = 4
 HALF = S // 2
-FIRST = 384
+FIRST = 256
 ROW0 = 112
 
 
@@ -32,49 +32,42 @@ def tile_list_tabscat_none_kernel(tc, tab, w, wgo, offs, offs2, out):
         scales = held.tile([P, T // 4], I32, name="scales", tag="scales", align_bytes=64)
         words = held.tile([P, T], I32, name="words", align_bytes=64)
         picked_scales = held.tile([P, S], U8, name="picked_scales", align_bytes=64)
-        windows = [held.tile([P, T], F32, name="window0", align_bytes=64)]
+        windows = [held.tile([P, T], F32, name=f"window{u}", align_bytes=64) for u in range(2)]
 
         nc.vector.memset(scales[0:ROW0, :], 0)
-        nc.vector.memset(picked_scales[:].bitcast(I32), 0)
-        nc.vector.memset(windows[0][:], 0.0)
+        for u in range(2):
+            nc.vector.memset(windows[u][:], 0.0)
 
         tab_words = tab[0, 0 : K * T].rearrange("(p b) -> p b", p=P).bitcast(I32)
         tab_scales = tab[0, K * T : K * T + 16 * T].rearrange("(q t) -> q t", q=16).bitcast(I32)
         w_rows = w.rearrange("(p j) c -> p j c", j=PACK)
-        w_chunks = ((0, 128), (128, 256), (256, 512))
-        raws = []
 
-        def load_w(i, queue, tag):
-            c0, c1 = w_chunks[i]
-            raws.append(held.tile([P, PACK, c1 - c0], F32, name=f"raw{c0}", tag=tag, align_bytes=64))
-            queue.dma_start(out=raws[i][:], in_=w_rows[:, :, c0:c1])
+        def load_w(c0, c1, queue, tag):
+            raw = held.tile([P, PACK, c1 - c0], F32, name=f"raw{c0}", tag=tag, align_bytes=64)
+            queue.dma_start(out=raw[:], in_=w_rows[:, :, c0:c1])
+            return raw
 
         nc.sync.dma_start(out=scales[ROW0:P, :], in_=tab_scales)
-        nc.sync.dma_start(offsets[:], offs)
-        nc.sync.dma_start(offsets2[:], offs2)
-        first_rows = [held.tile([P, 2, P], F32, name=f"first_rows{u}", tag=f"first_rows{u}", align_bytes=64) for u in range(2)]
-        raws.append(None)
-        nc.scalar.dma_start(out=first_rows[0][:], in_=w_rows[:, 0:2, 0:P])
         nc.scalar.dma_start(out=words[:], in_=tab_words)
-        nc.scalar.dma_start(out=first_rows[1][:], in_=w_rows[:, 2:4, 0:P])
+        nc.sync.dma_start(offsets[:], offs)
+        raw0 = load_w(0, P, nc.scalar, "raw0")
+        nc.sync.dma_start(offsets2[:], offs2)
+        raw1 = load_w(P, 2 * P, nc.scalar, "raw1")
+        weights_first = held.tile([P, FIRST], F32, name="weights_first", align_bytes=64)
+        nc.scalar.dma_start(out=weights_first[:], in_=wgo[:, 0:FIRST])
 
         codes = held.tile([P, M], U32, name="codes", align_bytes=64)
         planes = held.tile([P, M], U8, name="planes", align_bytes=64)
 
-        def prepare_w(i, a, b, tag):
-            c0 = w_chunks[i][0]
-            grouped = held.tile([P, b - a, PACK], BF16, name=f"grouped{a}", tag=tag, align_bytes=64)
-            if i == 0:
-                for u in range(2):
-                    nc.scalar.copy(
-                        out=grouped[:, :, 2 * u : 2 * u + 2].rearrange("p (c e) j -> p c j e", e=2),
-                        in_=first_rows[u][:].rearrange("p j (c e) -> p c j e", e=2),
-                    )
-            else:
-                nc.scalar.copy(
-                    out=grouped[:].rearrange("p (c e) j -> p c j e", e=2),
-                    in_=raws[i][:, :, a - c0 : b - c0].rearrange("p j (c e) -> p c j e", e=2),
-                )
+        def interleave(raw, a, b):
+            grouped = held.tile([P, b - a, PACK], BF16, name=f"grouped{a}", align_bytes=64)
+            nc.scalar.copy(
+                out=grouped[:].rearrange("p (c e) j -> p c j e", e=2),
+                in_=raw[:].rearrange("p j (c e) -> p c j e", e=2),
+            )
+            return grouped
+
+        def quantise(grouped, a, b):
             nc.vector.quantize_mx(
                 out=codes[:, a:b].bitcast(FP8X4),
                 scales=planes[:, a:b],
@@ -87,66 +80,71 @@ def tile_list_tabscat_none_kernel(tc, tab, w, wgo, offs, offs2, out):
         banks = [0]
         picked = []
 
-        def product(m, y, a, b):
+        def product(m, y, y0, a, b):
             acc = psum.tile([P, b - a], F32, name=f"acc{banks[0] % 8}")
             banks[0] += 1
-            h = 0 if a < FIRST else 1
+            h = a // HALF
             nc.tensor.matmul_mx(
                 out=acc[:],
                 lhsT=codes[:, m * P : (m + 1) * P].bitcast(FP8X4),
                 lhsT_scale=planes[:, m * P : (m + 1) * P],
-                rhs=picked[h][:, a - h * FIRST : b - h * FIRST].bitcast(FP8X4),
+                rhs=picked[h][:, a - h * HALF : b - h * HALF].bitcast(FP8X4),
                 rhs_scale=picked_scales[:, a:b],
                 start=True,
                 stop=True,
             )
-            nc.scalar.copy(out=y[:, a:b], in_=acc[:])
+            nc.scalar.copy(out=y[:, a - y0 : b - y0], in_=acc[:])
 
         def pick_scales(a, b, tag):
             rows = held.tile([P, b - a], U8, name=f"rows{a}", tag=tag, align_bytes=64)
             pick(rows[:], scales[:].bitcast(U8), a, b)
-            return rows
-
-        def carry(rows, a, b):
             for r in range(4):
                 nc.sync.dma_start(
                     out=picked_scales[r:P:32, a:b].bitcast(I32), in_=rows[ROW0 + r : P : 4, :].bitcast(I32)
                 )
 
-        ys = [held.tile([P, S], F32, name="y0")]
-        carry(pick_scales(0, FIRST, "rows_first"), 0, FIRST)
-        rows_rest = pick_scales(FIRST, S, "rows_rest")
-        weights_first = held.tile([P, FIRST], F32, name="weights_first", tag="scales", align_bytes=64)
-        nc.sync.dma_start(out=weights_first[:], in_=wgo[:, 0:FIRST])
-        carry(rows_rest, FIRST, S)
-        load_w(1, nc.sync, "rows_first")
+        def put(m, y, weight, a, b):
+            nc.vector.tensor_tensor(windows[m % 2][:].indirect(offsets2[:, a // 16 : b // 16]), y, weight, MULT)
 
-        picked.append(held.tile([P, FIRST], U32, name="picked0", align_bytes=64))
-        pick(picked[0][:], words[:].bitcast(U32), 0, FIRST)
-        prepare_w(0, 0, P, "staged")
-        weights = held.tile([P, S], F32, name="weights", tag="staged", align_bytes=64)
-        nc.sync.dma_start(out=weights[:], in_=wgo)
-        load_w(2, nc.sync, "rows_rest")
-        for a in range(0, FIRST, P):
-            product(0, ys[0], a, a + P)
-        picked.append(held.tile([P, S - FIRST], U32, name="picked1", tag="first_rows1", align_bytes=64))
-        pick(picked[1][:], words[:].bitcast(U32), FIRST, S)
-        product(0, ys[0], FIRST, FIRST + HALF)
-        product(0, ys[0], FIRST + HALF, S)
-        nc.vector.tensor_tensor(
-            windows[0][:].indirect(offsets2[:, 0 : FIRST // 16]), ys[0][:, 0:FIRST], weights_first[:], MULT
-        )
-        prepare_w(1, P, 2 * P, "grouped1")
-        windows.append(held.tile([P, T], F32, name="window1", tag="grouped1", align_bytes=64))
-        nc.gpsimd.memset(windows[1][:], 0.0)
-        prepare_w(2, 2 * P, M, "grouped2")
-        for m in range(4):
-            a = FIRST if m == 0 else 0
-            if m > 0:
-                ys.append(held.tile([P, S], F32, name=f"y{m}", tag="rows_rest" if m == 1 else f"y{m}", align_bytes=64))
-                for c, d in ((0, 256), (256, FIRST), (FIRST, FIRST + HALF), (FIRST + HALF, S)):
-                    product(m, ys[m], c, d)
-            nc.vector.tensor_tensor(
-                windows[m % 2][:].indirect(offsets2[:, a // 16 : S // 16]), ys[m][:, a:S], weights[:, a:S], MULT
-            )
+        def store(m):
             nc.sync.dma_start(out=out[m * P : (m + 1) * P, :], in_=windows[m % 2][:])
+
+        pick_scales(0, FIRST, "rows_first")
+        pick_scales(FIRST, S, "rows_rest")
+        weights = held.tile([P, S], F32, name="weights", tag="scales", align_bytes=64)
+        nc.sync.dma_start(out=weights[:], in_=wgo)
+        raw2 = load_w(2 * P, M, nc.sync, "rows_rest")
+
+        grouped0 = interleave(raw0, 0, P)
+        grouped1 = interleave(raw1, P, 2 * P)
+        picked.append(held.tile([P, HALF], U32, name="picked0", align_bytes=64))
+        pick(picked[0][:], words[:].bitcast(U32), 0, HALF)
+        quantise(grouped0, 0, P)
+        picked.append(held.tile([P, HALF], U32, name="picked1", tag="raw0", align_bytes=64))
+        pick(picked[1][:], words[:].bitcast(U32), HALF, S)
+        quantise(grouped1, P, 2 * P)
+
+        firsts = [held.tile([P, FIRST], F32, name=f"first{m}", align_bytes=64) for m in range(2)]
+        for m in range(2):
+            product(m, firsts[m], 0, 0, FIRST)
+            put(m, firsts[m][:], weights_first[:], 0, FIRST)
+
+        rest0 = held.tile([P, S - FIRST], F32, name="rest0", align_bytes=64)
+        product(0, rest0, FIRST, FIRST, HALF)
+        product(0, rest0, FIRST, HALF, S)
+        put(0, rest0[:], weights[:, FIRST:S], FIRST, S)
+        store(0)
+
+        quantise(interleave(raw2, 2 * P, M), 2 * P, M)
+        rest1 = held.tile([P, S - FIRST], F32, name="rest1", tag="rows_rest", align_bytes=64)
+        product(1, rest1, FIRST, FIRST, HALF)
+        product(1, rest1, FIRST, HALF, S)
+        put(1, rest1[:], weights[:, FIRST:S], FIRST, S)
+        store(1)
+
+        for m in range(2, 4):
+            y = held.tile([P, S], F32, name=f"y{m}", align_bytes=64)
+            product(m, y, 0, 0, HALF)
+            product(m, y, 0, HALF, S)
+            put(m, y[:], weights[:], 0, S)
+            store(m)

@@ -48,13 +48,16 @@ def tile_list_tabscat_none_kernel(tc, tab, w, wgo, offs, offs2, out):
             return raw
 
         nc.sync.dma_start(out=scales[ROW0:P, :], in_=tab_scales)
-        nc.scalar.dma_start(out=words[:], in_=tab_words)
+        row0 = held.tile([P, P], F32, name="row0", tag="row0", align_bytes=64)
+        nc.scalar.dma_start(out=row0[:], in_=w_rows[:, 0, 0:P])
         nc.sync.dma_start(offsets[:], offs)
-        raw0 = load_w(0, P, nc.scalar, "raw0")
+        nc.scalar.dma_start(out=words[:], in_=tab_words)
         nc.sync.dma_start(offsets2[:], offs2)
-        raw1 = load_w(P, 2 * P, nc.scalar, "raw1")
-        weights_first = held.tile([P, FIRST], F32, name="weights_first", align_bytes=64)
-        nc.scalar.dma_start(out=weights_first[:], in_=wgo[:, 0:FIRST])
+        rows123 = held.tile([P, PACK - 1, P], F32, name="rows123", tag="raw0", align_bytes=64)
+        nc.scalar.dma_start(out=rows123[:], in_=w_rows[:, 1:PACK, 0:P])
+        grouped0 = held.tile([P, P, PACK], BF16, name="grouped0", align_bytes=64)
+        nc.scalar.copy(out=grouped0[:, :, 0], in_=row0[:])
+        raw1 = load_w(P, 2 * P, nc.scalar, "row0")
 
         codes = held.tile([P, M], U32, name="codes", align_bytes=64)
         planes = held.tile([P, M], U8, name="planes", align_bytes=64)
@@ -98,6 +101,9 @@ def tile_list_tabscat_none_kernel(tc, tab, w, wgo, offs, offs2, out):
         def pick_scales(a, b, tag):
             rows = held.tile([P, b - a], U8, name=f"rows{a}", tag=tag, align_bytes=64)
             pick(rows[:], scales[:].bitcast(U8), a, b)
+            return rows
+
+        def carry(rows, a, b):
             for r in range(4):
                 nc.sync.dma_start(
                     out=picked_scales[r:P:32, a:b].bitcast(I32), in_=rows[ROW0 + r : P : 4, :].bitcast(I32)
@@ -109,13 +115,22 @@ def tile_list_tabscat_none_kernel(tc, tab, w, wgo, offs, offs2, out):
         def store(m):
             nc.sync.dma_start(out=out[m * P : (m + 1) * P, :], in_=windows[m % 2][:])
 
-        pick_scales(0, FIRST, "rows_first")
-        pick_scales(FIRST, S, "rows_rest")
-        weights = held.tile([P, S], F32, name="weights", tag="scales", align_bytes=64)
-        nc.sync.dma_start(out=weights[:], in_=wgo)
-        raw2 = load_w(2 * P, M, nc.sync, "rows_rest")
+        carry(pick_scales(0, FIRST, "rows_first"), 0, FIRST)
+        rows_rest = pick_scales(FIRST, S, "rows_rest")
+        weights_first = held.tile([P, FIRST], F32, name="weights_first", tag="scales", align_bytes=64)
+        nc.sync.dma_start(out=weights_first[:], in_=wgo[:, 0:FIRST])
+        carry(rows_rest, FIRST, S)
+        weights = held.tile([P, S], F32, name="weights", tag="rows_first", align_bytes=64)
+        nc.sync.dma_start(out=weights[:, FIRST:S], in_=wgo[:, FIRST:S])
+        nc.sync.dma_start(out=weights[:, 0:FIRST], in_=wgo[:, 0:FIRST])
+        raw2 = held.tile([P, PACK, 2 * P], F32, name="raw2", tag="rows_rest", align_bytes=64)
+        for u in range(2):
+            nc.sync.dma_start(out=raw2[:, 2 * u : 2 * u + 2, :], in_=w_rows[:, 2 * u : 2 * u + 2, 2 * P : M])
 
-        grouped0 = interleave(raw0, 0, P)
+        nc.scalar.copy(
+            out=grouped0[:, :, 1:PACK].rearrange("p (c e) j -> p c j e", e=2),
+            in_=rows123[:].rearrange("p j (c e) -> p c j e", e=2),
+        )
         grouped1 = interleave(raw1, P, 2 * P)
         picked.append(held.tile([P, HALF], U32, name="picked0", align_bytes=64))
         pick(picked[0][:], words[:].bitcast(U32), 0, HALF)

@@ -25,6 +25,7 @@ def tile_list_tabscat_none_kernel(tc, tab, w, wgo, offs, offs2, out):
     nc = tc.nc
     with ExitStack() as ctx:
         held = ctx.enter_context(tc.tile_pool(name="held", bufs=1))
+        placed = ctx.enter_context(tc.tile_pool(name="placed", bufs=1))
         psum = ctx.enter_context(tc.psum_pool(name="psum", bufs=1))
 
         offsets = held.tile([P, S // 16], U16, name="offsets")
@@ -42,22 +43,20 @@ def tile_list_tabscat_none_kernel(tc, tab, w, wgo, offs, offs2, out):
         tab_scales = tab[0, K * T : K * T + 16 * T].rearrange("(q t) -> q t", q=16).bitcast(I32)
         w_rows = w.rearrange("(p j) c -> p j c", j=PACK)
 
-        def load_w(c0, c1, queue, tag):
-            raw = held.tile([P, PACK, c1 - c0], F32, name=f"raw{c0}", tag=tag, align_bytes=64)
-            queue.dma_start(out=raw[:], in_=w_rows[:, :, c0:c1])
-            return raw
-
-        nc.sync.dma_start(out=scales[ROW0:P, :], in_=tab_scales)
-        row0 = held.tile([P, P], F32, name="row0", tag="row0", align_bytes=64)
-        nc.scalar.dma_start(out=row0[:], in_=w_rows[:, 0, 0:P])
+        nc.scalar.dma_start(out=scales[ROW0:P, :], in_=tab_scales)
         nc.sync.dma_start(offsets[:], offs)
-        nc.scalar.dma_start(out=words[:], in_=tab_words)
+        row0 = placed.tile([P, P], F32, name="row0", offset=1792)
+        nc.scalar.dma_start(out=row0[:], in_=w_rows[:, 0, 0:P])
         nc.sync.dma_start(offsets2[:], offs2)
+        nc.scalar.dma_start(out=words[:], in_=tab_words)
         rows123 = held.tile([P, PACK - 1, P], F32, name="rows123", tag="raw0", align_bytes=64)
         nc.scalar.dma_start(out=rows123[:], in_=w_rows[:, 1:PACK, 0:P])
         grouped0 = held.tile([P, P, PACK], BF16, name="grouped0", align_bytes=64)
         nc.scalar.copy(out=grouped0[:, :, 0], in_=row0[:])
-        raw1 = load_w(P, 2 * P, nc.scalar, "row0")
+        raw1 = placed.tile([P, PACK, P], F32, name="raw1", offset=0)
+        nc.scalar.dma_start(out=raw1[:], in_=w_rows[:, :, P : 2 * P])
+        weights_first = placed.tile([P, FIRST], F32, name="weights_first", offset=2048)
+        nc.scalar.dma_start(out=weights_first[:], in_=wgo[:, 0:FIRST])
 
         codes = held.tile([P, M], U32, name="codes", align_bytes=64)
         planes = held.tile([P, M], U8, name="planes", align_bytes=64)
@@ -117,8 +116,6 @@ def tile_list_tabscat_none_kernel(tc, tab, w, wgo, offs, offs2, out):
 
         carry(pick_scales(0, FIRST, "rows_first"), 0, FIRST)
         rows_rest = pick_scales(FIRST, S, "rows_rest")
-        weights_first = held.tile([P, FIRST], F32, name="weights_first", tag="scales", align_bytes=64)
-        nc.sync.dma_start(out=weights_first[:], in_=wgo[:, 0:FIRST])
         carry(rows_rest, FIRST, S)
         weights = held.tile([P, S], F32, name="weights", tag="rows_first", align_bytes=64)
         nc.sync.dma_start(out=weights[:, FIRST:S], in_=wgo[:, FIRST:S])

@@ -33,11 +33,10 @@ def tile_list_tabscat_none_kernel(tc, tab, w, wgo, offs, offs2, out):
         scales = held.tile([P, T // 4], I32, name="scales", tag="scales", align_bytes=64)
         words = held.tile([P, T], I32, name="words", align_bytes=64)
         picked_scales = held.tile([P, S], U8, name="picked_scales", align_bytes=64)
-        windows = [held.tile([P, T], F32, name=f"window{u}", align_bytes=64) for u in range(2)]
+        window0 = held.tile([P, T], F32, name="window0", align_bytes=64)
 
         nc.vector.memset(scales[0:ROW0, :], 0)
-        for u in range(2):
-            nc.vector.memset(windows[u][:], 0.0)
+        nc.vector.memset(window0[:], 0.0)
 
         tab_words = tab[0, 0 : K * T].rearrange("(p b) -> p b", p=P).bitcast(I32)
         tab_scales = tab[0, K * T : K * T + 16 * T].rearrange("(q t) -> q t", q=16).bitcast(I32)
@@ -45,24 +44,18 @@ def tile_list_tabscat_none_kernel(tc, tab, w, wgo, offs, offs2, out):
 
         nc.scalar.dma_start(out=scales[ROW0:P, :], in_=tab_scales)
         nc.sync.dma_start(offsets[:], offs)
-        row0 = placed.tile([P, P], F32, name="row0", offset=1792)
-        nc.scalar.dma_start(out=row0[:], in_=w_rows[:, 0, 0:P])
-        nc.sync.dma_start(offsets2[:], offs2)
         nc.scalar.dma_start(out=words[:], in_=tab_words)
-        rows123 = held.tile([P, PACK - 1, P], F32, name="rows123", tag="raw0", align_bytes=64)
-        nc.scalar.dma_start(out=rows123[:], in_=w_rows[:, 1:PACK, 0:P])
-        grouped0 = held.tile([P, P, PACK], BF16, name="grouped0", align_bytes=64)
-        nc.scalar.copy(out=grouped0[:, :, 0], in_=row0[:])
-        raw1 = placed.tile([P, PACK, P], F32, name="raw1", offset=0)
+        raw0 = placed.tile([P, PACK, P], F32, name="raw0", offset=0, align_bytes=64)
+        nc.sync.dma_start(out=raw0[:], in_=w_rows[:, :, 0:P])
+        nc.sync.dma_start(offsets2[:], offs2)
+        raw1 = held.tile([P, PACK, P], F32, name="raw1", tag="raw1", align_bytes=64)
         nc.scalar.dma_start(out=raw1[:], in_=w_rows[:, :, P : 2 * P])
-        weights_first = placed.tile([P, FIRST], F32, name="weights_first", offset=2048)
-        nc.scalar.dma_start(out=weights_first[:], in_=wgo[:, 0:FIRST])
 
         codes = held.tile([P, M], U32, name="codes", align_bytes=64)
         planes = held.tile([P, M], U8, name="planes", align_bytes=64)
 
         def interleave(raw, a, b):
-            grouped = held.tile([P, b - a, PACK], BF16, name=f"grouped{a}", align_bytes=64)
+            grouped = held.tile([P, b - a, PACK], BF16, name=f"grouped{a}", tag=f"grouped{a}", align_bytes=64)
             nc.scalar.copy(
                 out=grouped[:].rearrange("p (c e) j -> p c j e", e=2),
                 in_=raw[:].rearrange("p j (c e) -> p c j e", e=2),
@@ -79,23 +72,22 @@ def tile_list_tabscat_none_kernel(tc, tab, w, wgo, offs, offs2, out):
         def pick(dst, src, a, b):
             nc.vector.tensor_copy(out=dst, in_=src.indirect(offsets[:, a // 16 : b // 16]))
 
-        banks = [0]
         picked = []
 
-        def product(m, y, y0, a, b):
-            acc = psum.tile([P, b - a], F32, name=f"acc{banks[0] % 8}")
-            banks[0] += 1
-            h = a // HALF
-            nc.tensor.matmul_mx(
-                out=acc[:],
-                lhsT=codes[:, m * P : (m + 1) * P].bitcast(FP8X4),
-                lhsT_scale=planes[:, m * P : (m + 1) * P],
-                rhs=picked[h][:, a - h * HALF : b - h * HALF].bitcast(FP8X4),
-                rhs_scale=picked_scales[:, a:b],
-                start=True,
-                stop=True,
-            )
-            nc.scalar.copy(out=y[:, a - y0 : b - y0], in_=acc[:])
+        def product(m, y, cuts, bank):
+            acc = psum.tile([P, cuts[-1] - cuts[0]], F32, name=f"acc{bank}")
+            for a, b in zip(cuts, cuts[1:]):
+                h, base = (0, 0) if a < FIRST else (1, FIRST)
+                nc.tensor.matmul_mx(
+                    out=acc[:, a - cuts[0] : b - cuts[0]],
+                    lhsT=codes[:, m * P : (m + 1) * P].bitcast(FP8X4),
+                    lhsT_scale=planes[:, m * P : (m + 1) * P],
+                    rhs=picked[h][:, a - base : b - base].bitcast(FP8X4),
+                    rhs_scale=picked_scales[:, a:b],
+                    start=True,
+                    stop=True,
+                )
+            nc.scalar.copy(out=y, in_=acc[:])
 
         def pick_scales(a, b, tag):
             rows = held.tile([P, b - a], U8, name=f"rows{a}", tag=tag, align_bytes=64)
@@ -116,47 +108,48 @@ def tile_list_tabscat_none_kernel(tc, tab, w, wgo, offs, offs2, out):
 
         carry(pick_scales(0, FIRST, "rows_first"), 0, FIRST)
         rows_rest = pick_scales(FIRST, S, "rows_rest")
+        weights_first = held.tile([P, FIRST], F32, name="weights_first", tag="scales", align_bytes=64)
+        nc.sync.dma_start(out=weights_first[:], in_=wgo[:, 0:FIRST])
         carry(rows_rest, FIRST, S)
         weights = held.tile([P, S], F32, name="weights", tag="rows_first", align_bytes=64)
         nc.sync.dma_start(out=weights[:, FIRST:S], in_=wgo[:, FIRST:S])
         nc.sync.dma_start(out=weights[:, 0:FIRST], in_=wgo[:, 0:FIRST])
         raw2 = held.tile([P, PACK, 2 * P], F32, name="raw2", tag="rows_rest", align_bytes=64)
-        for u in range(2):
-            nc.sync.dma_start(out=raw2[:, 2 * u : 2 * u + 2, :], in_=w_rows[:, 2 * u : 2 * u + 2, 2 * P : M])
+        for j0, j1 in ((0, 2), (2, 3), (3, 4)):
+            nc.sync.dma_start(out=raw2[:, j0:j1, :], in_=w_rows[:, j0:j1, 2 * P : M])
 
-        nc.scalar.copy(
-            out=grouped0[:, :, 1:PACK].rearrange("p (c e) j -> p c j e", e=2),
-            in_=rows123[:].rearrange("p j (c e) -> p c j e", e=2),
-        )
-        grouped1 = interleave(raw1, P, 2 * P)
-        picked.append(held.tile([P, HALF], U32, name="picked0", align_bytes=64))
-        pick(picked[0][:], words[:].bitcast(U32), 0, HALF)
+        grouped0 = interleave(raw0, 0, P)
         quantise(grouped0, 0, P)
-        picked.append(held.tile([P, HALF], U32, name="picked1", tag="raw0", align_bytes=64))
-        pick(picked[1][:], words[:].bitcast(U32), HALF, S)
-        quantise(grouped1, P, 2 * P)
+        window1 = held.tile([P, T], F32, name="window1", tag="grouped0", align_bytes=64)
+        nc.gpsimd.memset(window1[:], 0.0)
+        windows = [window0, window1]
+        picked.append(placed.tile([P, FIRST], U32, name="picked0", offset=0, align_bytes=64))
+        pick(picked[0][:], words[:].bitcast(U32), 0, FIRST)
+        picked.append(placed.tile([P, S - FIRST], U32, name="picked1", offset=4 * FIRST, align_bytes=64))
+        pick(picked[1][:], words[:].bitcast(U32), FIRST, S)
+        quantise(interleave(raw1, P, 2 * P), P, 2 * P)
 
-        firsts = [held.tile([P, FIRST], F32, name=f"first{m}", align_bytes=64) for m in range(2)]
+        firsts = held.tile([P, 2, FIRST], F32, name="firsts", tag="raw1", align_bytes=64)
         for m in range(2):
-            product(m, firsts[m], 0, 0, FIRST)
-            put(m, firsts[m][:], weights_first[:], 0, FIRST)
+            product(m, firsts[:, m, :], (0, FIRST), m)
+            put(m, firsts[:, m, :], weights_first[:], 0, FIRST)
 
         rest0 = held.tile([P, S - FIRST], F32, name="rest0", align_bytes=64)
-        product(0, rest0, FIRST, FIRST, HALF)
-        product(0, rest0, FIRST, HALF, S)
+        product(0, rest0[:, 0:FIRST], (FIRST, HALF), 2)
+        product(0, rest0[:, FIRST : S - FIRST], (HALF, S), 3)
         put(0, rest0[:], weights[:, FIRST:S], FIRST, S)
         store(0)
 
         quantise(interleave(raw2, 2 * P, M), 2 * P, M)
         rest1 = held.tile([P, S - FIRST], F32, name="rest1", tag="rows_rest", align_bytes=64)
-        product(1, rest1, FIRST, FIRST, HALF)
-        product(1, rest1, FIRST, HALF, S)
+        product(1, rest1[:, 0:FIRST], (FIRST, HALF), 4)
+        product(1, rest1[:, FIRST : S - FIRST], (HALF, S), 5)
         put(1, rest1[:], weights[:, FIRST:S], FIRST, S)
         store(1)
 
         for m in range(2, 4):
             y = held.tile([P, S], F32, name=f"y{m}", align_bytes=64)
-            product(m, y, 0, 0, HALF)
-            product(m, y, 0, HALF, S)
+            product(m, y[:, 0:HALF], (0, FIRST, HALF), 6)
+            product(m, y[:, HALF:S], (HALF, S), 7)
             put(m, y[:], weights[:], 0, S)
             store(m)

@@ -25,15 +25,14 @@ def tile_list_tabscat_none_kernel(tc, tab, w, wgo, offs, offs2, out):
     nc = tc.nc
     with ExitStack() as ctx:
         held = ctx.enter_context(tc.tile_pool(name="held", bufs=1))
-        placed = ctx.enter_context(tc.tile_pool(name="placed", bufs=1))
         psum = ctx.enter_context(tc.psum_pool(name="psum", bufs=1))
 
         offsets = held.tile([P, S // 16], U16, name="offsets")
         offsets2 = held.tile([P, S // 16], U16, name="offsets2")
-        scales = held.tile([P, T // 4], I32, name="scales", tag="scales", align_bytes=64)
-        words = held.tile([P, T], I32, name="words", align_bytes=64)
-        picked_scales = held.tile([P, S], U8, name="picked_scales", align_bytes=64)
-        window0 = held.tile([P, T], F32, name="window0", align_bytes=64)
+        scales = held.tile([P, T // 4], I32, name="scales", tag="scales", align_bytes=256)
+        words = held.tile([P, T], I32, name="words", align_bytes=256)
+        picked_scales = held.tile([P, S], U8, name="picked_scales", align_bytes=256)
+        window0 = held.tile([P, T], F32, name="window0", align_bytes=256)
 
         nc.vector.memset(scales[0:ROW0, :], 0)
         nc.vector.memset(window0[:], 0.0)
@@ -44,18 +43,27 @@ def tile_list_tabscat_none_kernel(tc, tab, w, wgo, offs, offs2, out):
 
         nc.scalar.dma_start(out=scales[ROW0:P, :], in_=tab_scales)
         nc.sync.dma_start(offsets[:], offs)
-        nc.scalar.dma_start(out=words[:], in_=tab_words)
-        raw0 = placed.tile([P, PACK, P], F32, name="raw0", offset=0, align_bytes=64)
-        nc.sync.dma_start(out=raw0[:], in_=w_rows[:, :, 0:P])
+        nc.scalar.dma_start(out=words[:, 0 : T // 2], in_=tab_words[:, 0 : T // 2])
+        row0 = held.tile([P, P], F32, name="row0", tag="row0", align_bytes=256)
+        nc.sync.dma_start(out=row0[:], in_=w_rows[:, 0, 0:P])
+        nc.sync.dma_start(out=words[:, T // 2 : T], in_=tab_words[:, T // 2 : T])
+        rows123 = held.tile([P, PACK - 1, P], F32, name="rows123", tag="rows123", align_bytes=256)
+        nc.sync.dma_start(out=rows123[:], in_=w_rows[:, 1:PACK, 0:P])
         nc.sync.dma_start(offsets2[:], offs2)
-        raw1 = held.tile([P, PACK, P], F32, name="raw1", tag="raw1", align_bytes=64)
-        nc.scalar.dma_start(out=raw1[:], in_=w_rows[:, :, P : 2 * P])
+        raw1 = held.tile([P, PACK, P], F32, name="raw1", tag="raw1", align_bytes=256)
+        nc.sync.dma_start(out=raw1[:], in_=w_rows[:, :, P : 2 * P])
 
-        codes = held.tile([P, M], U32, name="codes", align_bytes=64)
-        planes = held.tile([P, M], U8, name="planes", align_bytes=64)
+        grouped0 = held.tile([P, P, PACK], BF16, name="grouped0", align_bytes=256)
+        nc.scalar.copy(out=grouped0[:, :, 0], in_=row0[:])
+        window1 = held.tile([P, T], F32, name="window1", tag="row0", align_bytes=256)
+        nc.gpsimd.memset(window1[:], 0.0)
+        windows = [window0, window1]
+
+        codes = held.tile([P, M], U32, name="codes", align_bytes=256)
+        planes = held.tile([P, M], U8, name="planes", align_bytes=256)
 
         def interleave(raw, a, b):
-            grouped = held.tile([P, b - a, PACK], BF16, name=f"grouped{a}", tag=f"grouped{a}", align_bytes=64)
+            grouped = held.tile([P, b - a, PACK], BF16, name=f"grouped{a}", tag=f"grouped{a}", align_bytes=256)
             nc.scalar.copy(
                 out=grouped[:].rearrange("p (c e) j -> p c j e", e=2),
                 in_=raw[:].rearrange("p j (c e) -> p c j e", e=2),
@@ -77,7 +85,7 @@ def tile_list_tabscat_none_kernel(tc, tab, w, wgo, offs, offs2, out):
         def product(m, y, cuts, bank):
             acc = psum.tile([P, cuts[-1] - cuts[0]], F32, name=f"acc{bank}")
             for a, b in zip(cuts, cuts[1:]):
-                h, base = (0, 0) if a < FIRST else (1, FIRST)
+                h, base = (0, 0) if a < HALF else (1, HALF)
                 nc.tensor.matmul_mx(
                     out=acc[:, a - cuts[0] : b - cuts[0]],
                     lhsT=codes[:, m * P : (m + 1) * P].bitcast(FP8X4),
@@ -90,7 +98,7 @@ def tile_list_tabscat_none_kernel(tc, tab, w, wgo, offs, offs2, out):
             nc.scalar.copy(out=y, in_=acc[:])
 
         def pick_scales(a, b, tag):
-            rows = held.tile([P, b - a], U8, name=f"rows{a}", tag=tag, align_bytes=64)
+            rows = held.tile([P, b - a], U8, name=f"rows{a}", tag=tag, align_bytes=256)
             pick(rows[:], scales[:].bitcast(U8), a, b)
             return rows
 
@@ -108,48 +116,47 @@ def tile_list_tabscat_none_kernel(tc, tab, w, wgo, offs, offs2, out):
 
         carry(pick_scales(0, FIRST, "rows_first"), 0, FIRST)
         rows_rest = pick_scales(FIRST, S, "rows_rest")
-        weights_first = held.tile([P, FIRST], F32, name="weights_first", tag="scales", align_bytes=64)
+        weights_first = held.tile([P, FIRST], F32, name="weights_first", tag="scales", align_bytes=256)
         nc.sync.dma_start(out=weights_first[:], in_=wgo[:, 0:FIRST])
         carry(rows_rest, FIRST, S)
-        weights = held.tile([P, S], F32, name="weights", tag="rows_first", align_bytes=64)
+        weights = held.tile([P, S], F32, name="weights", tag="rows_first", align_bytes=256)
         nc.sync.dma_start(out=weights[:, FIRST:S], in_=wgo[:, FIRST:S])
         nc.sync.dma_start(out=weights[:, 0:FIRST], in_=wgo[:, 0:FIRST])
-        raw2 = held.tile([P, PACK, 2 * P], F32, name="raw2", tag="rows_rest", align_bytes=64)
-        for j0, j1 in ((0, 2), (2, 3), (3, 4)):
-            nc.sync.dma_start(out=raw2[:, j0:j1, :], in_=w_rows[:, j0:j1, 2 * P : M])
+        raw2 = held.tile([P, PACK, 2 * P], F32, name="raw2", tag="rows_rest", align_bytes=256)
+        nc.sync.dma_start(out=raw2[:], in_=w_rows[:, :, 2 * P : M])
 
-        grouped0 = interleave(raw0, 0, P)
+        nc.scalar.copy(
+            out=grouped0[:, :, 1:PACK].rearrange("p (c e) j -> p c j e", e=2),
+            in_=rows123[:].rearrange("p j (c e) -> p c j e", e=2),
+        )
+        picked.append(held.tile([P, HALF], U32, name="picked0", align_bytes=256))
+        pick(picked[0][:], words[:].bitcast(U32), 0, HALF)
         quantise(grouped0, 0, P)
-        window1 = held.tile([P, T], F32, name="window1", tag="grouped0", align_bytes=64)
-        nc.gpsimd.memset(window1[:], 0.0)
-        windows = [window0, window1]
-        picked.append(placed.tile([P, FIRST], U32, name="picked0", offset=0, align_bytes=64))
-        pick(picked[0][:], words[:].bitcast(U32), 0, FIRST)
-        picked.append(placed.tile([P, S - FIRST], U32, name="picked1", offset=4 * FIRST, align_bytes=64))
-        pick(picked[1][:], words[:].bitcast(U32), FIRST, S)
+        picked.append(held.tile([P, HALF], U32, name="picked1", tag="rows123", align_bytes=256))
+        pick(picked[1][:], words[:].bitcast(U32), HALF, S)
         quantise(interleave(raw1, P, 2 * P), P, 2 * P)
 
-        firsts = held.tile([P, 2, FIRST], F32, name="firsts", tag="raw1", align_bytes=64)
+        firsts = held.tile([P, 2, FIRST], F32, name="firsts", tag="raw1", align_bytes=256)
         for m in range(2):
             product(m, firsts[:, m, :], (0, FIRST), m)
             put(m, firsts[:, m, :], weights_first[:], 0, FIRST)
 
-        rest0 = held.tile([P, S - FIRST], F32, name="rest0", align_bytes=64)
+        rest0 = held.tile([P, S - FIRST], F32, name="rest0", align_bytes=256)
         product(0, rest0[:, 0:FIRST], (FIRST, HALF), 2)
         product(0, rest0[:, FIRST : S - FIRST], (HALF, S), 3)
         put(0, rest0[:], weights[:, FIRST:S], FIRST, S)
         store(0)
 
         quantise(interleave(raw2, 2 * P, M), 2 * P, M)
-        rest1 = held.tile([P, S - FIRST], F32, name="rest1", tag="rows_rest", align_bytes=64)
+        rest1 = held.tile([P, S - FIRST], F32, name="rest1", tag="rows_rest", align_bytes=256)
         product(1, rest1[:, 0:FIRST], (FIRST, HALF), 4)
         product(1, rest1[:, FIRST : S - FIRST], (HALF, S), 5)
         put(1, rest1[:], weights[:, FIRST:S], FIRST, S)
         store(1)
 
         for m in range(2, 4):
-            y = held.tile([P, S], F32, name=f"y{m}", align_bytes=64)
-            product(m, y[:, 0:HALF], (0, FIRST, HALF), 6)
+            y = held.tile([P, S], F32, name=f"y{m}", align_bytes=256)
+            product(m, y[:, 0:HALF], (0, HALF), 6)
             product(m, y[:, HALF:S], (HALF, S), 7)
             put(m, y[:], weights[:], 0, S)
             store(m)

@@ -49,9 +49,9 @@ def tile_list_tabscat_none_kernel(tc, tab, w, wgo, offs, offs2, out):
         nc.sync.dma_start(out=words[:, T // 2 : T], in_=tab_words[:, T // 2 : T])
         rows123 = held.tile([P, PACK - 1, P], F32, name="rows123", tag="rows123", align_bytes=256)
         nc.sync.dma_start(out=rows123[:], in_=w_rows[:, 1:PACK, 0:P])
-        nc.sync.dma_start(offsets2[:], offs2)
         raw1 = held.tile([P, PACK, P], F32, name="raw1", tag="raw1", align_bytes=256)
         nc.sync.dma_start(out=raw1[:], in_=w_rows[:, :, P : 2 * P])
+        nc.sync.dma_start(offsets2[:], offs2)
 
         grouped0 = held.tile([P, P, PACK], BF16, name="grouped0", align_bytes=256)
         nc.scalar.copy(out=grouped0[:, :, 0], in_=row0[:])
@@ -138,7 +138,8 @@ def tile_list_tabscat_none_kernel(tc, tab, w, wgo, offs, offs2, out):
 
         firsts = held.tile([P, 2, FIRST], F32, name="firsts", tag="raw1", align_bytes=256)
         for m in range(2):
-            product(m, firsts[:, m, :], (0, FIRST), m)
+            for u in range(2):
+                product(m, firsts[:, m, u * P : (u + 1) * P], (u * P, (u + 1) * P), u)
             put(m, firsts[:, m, :], weights_first[:], 0, FIRST)
 
         rest0 = held.tile([P, S - FIRST], F32, name="rest0", align_bytes=256)

@@ -18,6 +18,7 @@ P = 128
 PACK = 4
 HALF = S // 2
 FIRST = 256
+SPLIT = 768
 ROW0 = 112
 
 
@@ -43,15 +44,12 @@ def tile_list_tabscat_none_kernel(tc, tab, w, wgo, offs, offs2, out):
 
         nc.scalar.dma_start(out=scales[ROW0:P, :], in_=tab_scales)
         nc.sync.dma_start(offsets[:], offs)
-        nc.scalar.dma_start(out=words[:, 0 : T // 2], in_=tab_words[:, 0 : T // 2])
+        nc.scalar.dma_start(out=words[:, 0:SPLIT], in_=tab_words[:, 0:SPLIT])
         row0 = held.tile([P, P], F32, name="row0", tag="row0", align_bytes=256)
         nc.sync.dma_start(out=row0[:], in_=w_rows[:, 0, 0:P])
-        nc.sync.dma_start(out=words[:, T // 2 : T], in_=tab_words[:, T // 2 : T])
+        nc.sync.dma_start(out=words[:, SPLIT:T], in_=tab_words[:, SPLIT:T])
         rows123 = held.tile([P, PACK - 1, P], F32, name="rows123", tag="rows123", align_bytes=256)
         nc.sync.dma_start(out=rows123[:], in_=w_rows[:, 1:PACK, 0:P])
-        raw1 = held.tile([P, PACK, P], F32, name="raw1", tag="raw1", align_bytes=256)
-        nc.sync.dma_start(out=raw1[:], in_=w_rows[:, :, P : 2 * P])
-        nc.sync.dma_start(offsets2[:], offs2)
 
         grouped0 = held.tile([P, P, PACK], BF16, name="grouped0", align_bytes=256)
         nc.scalar.copy(out=grouped0[:, :, 0], in_=row0[:])
@@ -115,13 +113,16 @@ def tile_list_tabscat_none_kernel(tc, tab, w, wgo, offs, offs2, out):
             nc.sync.dma_start(out=out[m * P : (m + 1) * P, :], in_=windows[m % 2][:])
 
         carry(pick_scales(0, FIRST, "rows_first"), 0, FIRST)
+        raw1 = held.tile([P, PACK, P], F32, name="raw1", tag="raw1", align_bytes=256)
+        for j in range(0, PACK, 2):
+            nc.sync.dma_start(out=raw1[:, j : j + 2, :], in_=w_rows[:, j : j + 2, P : 2 * P])
         rows_rest = pick_scales(FIRST, S, "rows_rest")
         weights_first = held.tile([P, FIRST], F32, name="weights_first", tag="scales", align_bytes=256)
         nc.sync.dma_start(out=weights_first[:], in_=wgo[:, 0:FIRST])
+        nc.sync.dma_start(offsets2[:], offs2)
         carry(rows_rest, FIRST, S)
         weights = held.tile([P, S], F32, name="weights", tag="rows_first", align_bytes=256)
-        nc.sync.dma_start(out=weights[:, FIRST:S], in_=wgo[:, FIRST:S])
-        nc.sync.dma_start(out=weights[:, 0:FIRST], in_=wgo[:, 0:FIRST])
+        nc.sync.dma_start(out=weights[:], in_=wgo)
         raw2 = held.tile([P, PACK, 2 * P], F32, name="raw2", tag="rows_rest", align_bytes=256)
         nc.sync.dma_start(out=raw2[:], in_=w_rows[:, :, 2 * P : M])
 
@@ -134,7 +135,13 @@ def tile_list_tabscat_none_kernel(tc, tab, w, wgo, offs, offs2, out):
         quantise(grouped0, 0, P)
         picked.append(held.tile([P, HALF], U32, name="picked1", tag="rows123", align_bytes=256))
         pick(picked[1][:], words[:].bitcast(U32), HALF, S)
-        quantise(interleave(raw1, P, 2 * P), P, 2 * P)
+        grouped1 = held.tile([P, P, PACK], BF16, name="grouped1", align_bytes=256)
+        for j in range(0, PACK, 2):
+            nc.scalar.copy(
+                out=grouped1[:, :, j : j + 2].rearrange("p (c e) j -> p c j e", e=2),
+                in_=raw1[:, j : j + 2, :].rearrange("p j (c e) -> p c j e", e=2),
+            )
+        quantise(grouped1, P, 2 * P)
 
         firsts = held.tile([P, 2, FIRST], F32, name="firsts", tag="raw1", align_bytes=256)
         for m in range(2):

from contextlib import ExitStack

import concourse.mybir as mybir

K, M, T, S = 512, 512, 2048, 1024
FLOPS = 2 * K * M * S

F32 = mybir.dt.float32
BF16 = mybir.dt.bfloat16
I32 = mybir.dt.int32
U32 = mybir.dt.uint32
U16 = mybir.dt.uint16
U8 = mybir.dt.uint8
FP8X4 = mybir.dt.float8_e4m3fn_x4
MULT = mybir.AluOpType.mult

P = 128
PACK = 4
HALF = S // 2
FIRST = 256
SPLIT = 768
ROW0 = 112


def tile_list_tabscat_none_kernel(tc, tab, w, wgo, offs, offs2, out):
    nc = tc.nc
    with ExitStack() as ctx:
        held = ctx.enter_context(tc.tile_pool(name="held", bufs=1))
        psum = ctx.enter_context(tc.psum_pool(name="psum", bufs=1))

        offsets = held.tile([P, S // 16], U16, name="offsets")
        offsets2 = held.tile([P, S // 16], U16, name="offsets2")
        scales = held.tile([P, T // 4], I32, name="scales", tag="scales", align_bytes=256)
        words = held.tile([P, T], I32, name="words", align_bytes=256)
        picked_scales = held.tile([P, S], U8, name="picked_scales", align_bytes=256)
        window0 = held.tile([P, T], F32, name="window0", align_bytes=256)

        nc.vector.memset(scales[0:ROW0, :], 0)
        nc.vector.memset(window0[:], 0.0)

        tab_words = tab[0, 0 : K * T].rearrange("(p b) -> p b", p=P).bitcast(I32)
        tab_scales = tab[0, K * T : K * T + 16 * T].rearrange("(q t) -> q t", q=16).bitcast(I32)
        w_rows = w.rearrange("(p j) c -> p j c", j=PACK)

        nc.scalar.dma_start(out=scales[ROW0:P, :], in_=tab_scales)
        nc.sync.dma_start(offsets[:], offs)
        nc.scalar.dma_start(out=words[:, 0:SPLIT], in_=tab_words[:, 0:SPLIT])
        row0 = held.tile([P, P], F32, name="row0", tag="row0", align_bytes=256)
        nc.sync.dma_start(out=row0[:], in_=w_rows[:, 0, 0:P])
        nc.sync.dma_start(out=words[:, SPLIT:T], in_=tab_words[:, SPLIT:T])
        rows123 = held.tile([P, PACK - 1, P], F32, name="rows123", tag="rows123", align_bytes=256)
        nc.sync.dma_start(out=rows123[:], in_=w_rows[:, 1:PACK, 0:P])

        grouped0 = held.tile([P, P, PACK], BF16, name="grouped0", align_bytes=256)
        nc.scalar.copy(out=grouped0[:, :, 0], in_=row0[:])
        window1 = held.tile([P, T], F32, name="window1", tag="row0", align_bytes=256)
        nc.gpsimd.memset(window1[:], 0.0)
        windows = [window0, window1]

        codes = held.tile([P, M], U32, name="codes", align_bytes=256)
        planes = held.tile([P, M], U8, name="planes", align_bytes=256)

        def interleave(raw, a, b):
            grouped = held.tile([P, b - a, PACK], BF16, name=f"grouped{a}", tag=f"grouped{a}", align_bytes=256)
            nc.scalar.copy(
                out=grouped[:].rearrange("p (c e) j -> p c j e", e=2),
                in_=raw[:].rearrange("p j (c e) -> p c j e", e=2),
            )
            return grouped

        def quantise(grouped, a, b):
            nc.vector.quantize_mx(
                out=codes[:, a:b].bitcast(FP8X4),
                scales=planes[:, a:b],
                in_=grouped[:].rearrange("p c j -> p (c j)"),
            )

        def pick(dst, src, a, b):
            nc.vector.tensor_copy(out=dst, in_=src.indirect(offsets[:, a // 16 : b // 16]))

        picked = []

        def product(m, y, cuts, bank):
            acc = psum.tile([P, cuts[-1] - cuts[0]], F32, name=f"acc{bank}")
            for a, b in zip(cuts, cuts[1:]):
                h, base = (0, 0) if a < HALF else (1, HALF)
                nc.tensor.matmul_mx(
                    out=acc[:, a - cuts[0] : b - cuts[0]],
                    lhsT=codes[:, m * P : (m + 1) * P].bitcast(FP8X4),
                    lhsT_scale=planes[:, m * P : (m + 1) * P],
                    rhs=picked[h][:, a - base : b - base].bitcast(FP8X4),
                    rhs_scale=picked_scales[:, a:b],
                    start=True,
                    stop=True,
                )
            nc.scalar.copy(out=y, in_=acc[:])

        def pick_scales(a, b, tag):
            rows = held.tile([P, b - a], U8, name=f"rows{a}", tag=tag, align_bytes=256)
            pick(rows[:], scales[:].bitcast(U8), a, b)
            return rows

        def carry(rows, a, b):
            for r in range(4):
                nc.sync.dma_start(
                    out=picked_scales[r:P:32, a:b].bitcast(I32), in_=rows[ROW0 + r : P : 4, :].bitcast(I32)
                )

        def put(m, y, weight, a, b):
            nc.vector.tensor_tensor(windows[m % 2][:].indirect(offsets2[:, a // 16 : b // 16]), y, weight, MULT)

        def store(m):
            nc.sync.dma_start(out=out[m * P : (m + 1) * P, :], in_=windows[m % 2][:])

        carry(pick_scales(0, FIRST, "rows_first"), 0, FIRST)
        raw1 = held.tile([P, PACK, P], F32, name="raw1", tag="raw1", align_bytes=256)
        for j in range(0, PACK, 2):
            nc.sync.dma_start(out=raw1[:, j : j + 2, :], in_=w_rows[:, j : j + 2, P : 2 * P])
        rows_rest = pick_scales(FIRST, S, "rows_rest")
        weights_first = held.tile([P, FIRST], F32, name="weights_first", tag="scales", align_bytes=256)
        nc.sync.dma_start(out=weights_first[:], in_=wgo[:, 0:FIRST])
        nc.sync.dma_start(offsets2[:], offs2)
        carry(rows_rest, FIRST, S)
        weights = held.tile([P, S], F32, name="weights", tag="rows_first", align_bytes=256)
        nc.sync.dma_start(out=weights[:], in_=wgo)
        raw2 = held.tile([P, PACK, 2 * P], F32, name="raw2", tag="rows_rest", align_bytes=256)
        nc.sync.dma_start(out=raw2[:], in_=w_rows[:, :, 2 * P : M])

        nc.scalar.copy(
            out=grouped0[:, :, 1:PACK].rearrange("p (c e) j -> p c j e", e=2),
            in_=rows123[:].rearrange("p j (c e) -> p c j e", e=2),
        )
        picked.append(held.tile([P, HALF], U32, name="picked0", align_bytes=256))
        pick(picked[0][:], words[:].bitcast(U32), 0, HALF)
        quantise(grouped0, 0, P)
        picked.append(held.tile([P, HALF], U32, name="picked1", tag="rows123", align_bytes=256))
        pick(picked[1][:], words[:].bitcast(U32), HALF, S)
        grouped1 = held.tile([P, P, PACK], BF16, name="grouped1", align_bytes=256)
        for j in range(0, PACK, 2):
            nc.scalar.copy(
                out=grouped1[:, :, j : j + 2].rearrange("p (c e) j -> p c j e", e=2),
                in_=raw1[:, j : j + 2, :].rearrange("p j (c e) -> p c j e", e=2),
            )
        quantise(grouped1, P, 2 * P)

        firsts = held.tile([P, 2, FIRST], F32, name="firsts", tag="raw1", align_bytes=256)
        for m in range(2):
            for u in range(2):
                product(m, firsts[:, m, u * P : (u + 1) * P], (u * P, (u + 1) * P), u)
            put(m, firsts[:, m, :], weights_first[:], 0, FIRST)

        rest0 = held.tile([P, S - FIRST], F32, name="rest0", align_bytes=256)
        product(0, rest0[:, 0:FIRST], (FIRST, HALF), 2)
        product(0, rest0[:, FIRST : S - FIRST], (HALF, S), 3)
        put(0, rest0[:], weights[:, FIRST:S], FIRST, S)
        store(0)

        quantise(interleave(raw2, 2 * P, M), 2 * P, M)
        rest1 = held.tile([P, S - FIRST], F32, name="rest1", tag="rows_rest", align_bytes=256)
        product(1, rest1[:, 0:FIRST], (FIRST, HALF), 4)
        product(1, rest1[:, FIRST : S - FIRST], (HALF, S), 5)
        put(1, rest1[:], weights[:, FIRST:S], FIRST, S)
        store(1)

        for m in range(2, 4):
            y = held.tile([P, S], F32, name=f"y{m}", align_bytes=256)
            product(m, y[:, 0:HALF], (0, HALF), 6)
            product(m, y[:, HALF:S], (HALF, S), 7)
            put(m, y[:], weights[:], 0, S)
            store(m)
